import numpy as np
import ml_dtypes


def mxq(x, axis, fmt="e4m3"):
    dtype, down = {"e4m3": (ml_dtypes.float8_e4m3fn, 7), "e5m2": (ml_dtypes.float8_e5m2, 14)}[fmt]
    v = np.moveaxis(np.asarray(x, np.float32).astype(ml_dtypes.bfloat16).astype(np.float64), axis, -1)
    blocks = v.reshape(v.shape[:-1] + (-1, 32))
    amax = np.abs(blocks).max(-1, keepdims=True)
    byte = np.maximum(np.where(amax > 0, np.frexp(amax)[1] - 1 + 127, 0) - down, 1)
    scale = np.exp2(byte - 127.0)
    codes = (blocks / scale).astype(np.float32).astype(dtype).astype(np.float64)
    return np.moveaxis((codes * scale).reshape(v.shape), -1, axis)


WIDE = False


def mx_kscale(k):
    if not WIDE:
        return np.ones(k)
    levels = np.array([10, -10, 5, -5, 0])
    if k % 512:
        return np.exp2(np.random.permutation(np.resize(levels, k // 32))).repeat(32)
    a = np.empty((k // 512, 16))
    for p in range(k // 512):
        a[p, :8] = np.random.permutation(np.resize(levels, 8))
        for g in range(8):
            far = levels[np.abs(levels - a[p, g]) >= 10]
            a[p, g + 8] = far[np.random.randint(len(far))]
    return np.exp2(a.ravel()).repeat(32)


def f64(x):
    return np.asarray(x).astype(np.float64)


def striped(idx):
    return np.tile(idx.reshape(-1, 16).T, (8, 1)).astype(np.uint16)


def unstriped(offs):
    return offs[:16].T.reshape(-1).astype(np.int64)


E2M1 = np.array([0.0, 0.5, 1.0, 1.5, 2.0, 3.0, 4.0, 6.0, -0.0, -0.5, -1.0, -1.5, -2.0, -3.0, -4.0, -6.0])


def pack_weight(w, fmt):
    k, n = w.shape
    w = f64(np.asarray(w, np.float32).astype(ml_dtypes.bfloat16)).reshape(k // 32, 32, n)
    amax = np.abs(w).max(1)
    if fmt == "e4m3":
        byte = np.frexp(amax)[1] - 1 + 127 - 7
    else:
        mant, ex = np.frexp(amax / 6.0)
        byte = np.where(mant > 0.5, ex, ex - 1) + 127
    byte = np.clip(np.where(amax > 0, byte, 1), 1, 254)
    scaled = (w * np.exp2(127.0 - byte)[:, None, :]).reshape(k, n).astype(np.float32)
    by_word = np.ascontiguousarray(scaled.reshape(k // 512, 128, 4, n).transpose(0, 1, 3, 2))
    if fmt == "e4m3":
        words = by_word.astype(ml_dtypes.float8_e4m3fn).view(np.uint8)
    else:
        c = by_word.astype(ml_dtypes.float4_e2m1fn).view(np.uint8) & 0xF
        words = (c[..., 0::2] | (c[..., 1::2] << 4)).reshape(k // 512, 128, 2 * n)
    return np.ascontiguousarray(words), np.ascontiguousarray(byte.astype(np.uint8).reshape(k // 512, 16, n))


def unpack_weight(words, scales, fmt):
    g, _, n = scales.shape
    words = np.ascontiguousarray(words).reshape(g, 128, n, -1)
    if fmt == "e4m3":
        vals = words.view(ml_dtypes.float8_e4m3fn).astype(np.float64)
    else:
        nib = np.empty((g, 128, n, 4), np.uint8)
        nib[..., 0::2] = words & 0xF
        nib[..., 1::2] = words >> 4
        vals = E2M1[nib]
    vals = vals * np.repeat(np.exp2(scales.astype(np.float64) - 127.0), 8, axis=1)[..., None]
    return vals.transpose(0, 1, 3, 2).reshape(g * 512, n)


def gelu(v):
    return 0.5 * v * (1.0 + np.tanh(np.sqrt(2.0 / np.pi) * (v + 0.044715 * v**3)))


K, T, E, C, H, N = 512, 768, 4, 256, 512, 128
PAD = 32


def by_expert(wq, xq):
    return np.concatenate([wq[e].T @ xq[:, e * C:(e + 1) * C] for e in range(E)], axis=1)


def setup_inputs():
    n = np.random.standard_normal
    s = mx_kscale(K)[:, None]
    u = mx_kscale(H)
    first = np.random.permutation(np.repeat(np.arange(E), T // E))
    second = (first + 1 + np.random.permutation(np.repeat(np.arange(E - 1), -(-T // (E - 1)))[:T])) % E
    while np.bincount(second, minlength=E).max() != T // E:
        load = np.bincount(second, minlength=E); hi, lo = int(load.argmax()), int(load.argmin())
        t = np.flatnonzero((second == hi) & (first != lo))[0]; second[t] = lo
    slot_token = np.empty(E * C, np.int64); pos = np.empty((2, T), np.int64); fill = np.zeros(E, np.int64)
    place = np.stack([np.random.permutation(C) for _ in range(E)])
    for r, deal in enumerate((first, second)):
        for t in np.random.permutation(T):
            e = deal[t]
            if fill[e] < C: j = e * C + place[e, fill[e]]; fill[e] += 1; slot_token[j] = t; pos[r, t] = j
            else: pos[r, t] = E * C + t % PAD
    g = np.random.uniform(0.2, 0.8, T)
    w1 = [pack_weight(m, "e2m1") for m in n((E, K, H)) / np.sqrt(K) / s[None] * u[None, None, :]]
    w2 = [pack_weight(m, "e2m1") for m in n((E, H, N)) / np.sqrt(H) / u[None, :, None]]
    return {
        "xT": (n((K, T)) * s).astype(np.float32),
        "w1_words": np.stack([m[0] for m in w1]),
        "w1_scales": np.stack([m[1] for m in w1]),
        "w2_words": np.stack([m[0] for m in w2]),
        "w2_scales": np.stack([m[1] for m in w2]),
        "gate": np.stack([np.tile(g, (N, 1)), np.tile(1.0 - g, (N, 1))]).astype(np.float32),
        "offs": striped(slot_token),
        "pos1": striped(pos[0]),
        "pos2": striped(pos[1]),
    }


def reference(xT, w1_words, w1_scales, w2_words, w2_scales, gate, offs, pos1, pos2):
    idx = unstriped(offs)
    w1 = np.stack([unpack_weight(w1_words[e], w1_scales[e], "e2m1") for e in range(E)])
    w2 = np.stack([unpack_weight(w2_words[e], w2_scales[e], "e2m1") for e in range(E)])
    xq = mxq(f64(xT)[:, idx], 0, "e4m3")
    h = gelu(by_expert(w1, xq))
    y = by_expert(w2, mxq(h, 0, "e4m3"))
    y = np.concatenate([y, np.zeros((N, PAD))], axis=1)
    return f64(gate[0]) * y[:, unstriped(pos1)] + f64(gate[1]) * y[:, unstriped(pos2)]

@@ -1,0 +1,200 @@
+from contextlib import ExitStack
+
+import concourse.mybir as mybir
+
+K, T, E, C, H, N = 512, 768, 4, 256, 512, 128
+PAD = 32
+S = E * C
+P = 128
+U = 128
+
+F32 = mybir.dt.float32
+BF16 = mybir.dt.bfloat16
+I32 = mybir.dt.int32
+U32 = mybir.dt.uint32
+U16 = mybir.dt.uint16
+U8 = mybir.dt.uint8
+FP8X4 = mybir.dt.float8_e4m3fn_x4
+FP4X4 = mybir.dt.float4_e2m1fn_x4
+ACT = mybir.ActivationFunctionType
+ALU = mybir.AluOpType
+
+FLOPS = 2 * S * (K * H + H * N)
+
+
+def tile_moe_cap2_mlp_gelu_kernel(tc, xT, w1_words, w1_scales, w2_words, w2_scales, gate, offs, pos1, pos2, out):
+    nc = tc.nc
+    with ExitStack() as ctx:
+        keep = ctx.enter_context(tc.tile_pool(name="keep", bufs=1))
+        apsum = ctx.enter_context(tc.psum_pool(name="apsum", bufs=6))
+        ypsum = ctx.enter_context(tc.psum_pool(name="ypsum", bufs=1))
+
+        offs_sb = keep.tile([P, S // 16], U16, name="offs_sb")
+        pos1_sb = keep.tile([P, T // 16], U16, name="pos1_sb")
+        pos2_sb = keep.tile([P, T // 16], U16, name="pos2_sb")
+        x_raw = keep.tile([P, 4, T], F32, name="x_raw")
+        x_bf = keep.tile([P, T, 4], BF16, name="x_bf", align_bytes=64)
+        x_codes = keep.tile([P, T], U32, name="x_codes", align_bytes=64)
+        x_scales = keep.tile([P, T], U8, name="x_scales", align_bytes=64)
+        w1_raw = keep.tile([P, E, 2 * H], U8, name="w1_raw", align_bytes=64)
+        w1_perm = keep.tile([P, E, 2 * H], U8, name="w1_perm", align_bytes=64)
+        s1_raw = keep.tile([P, H], U8, name="s1_raw", align_bytes=64)
+        s1_perm = keep.tile([P, H], U8, name="s1_perm", align_bytes=64)
+        s1_planes = [s1_perm] + [keep.tile([P, H], U8, name="s1_plane%d" % e, align_bytes=64) for e in range(1, E)]
+        w2_sb = keep.tile([P, E, 2 * N], U8, name="w2_sb", align_bytes=64)
+        s2_sb = keep.tile([P, E, N], U8, name="s2_sb", align_bytes=64)
+        gate_sb = keep.tile([P, 2, T], F32, name="gate_sb")
+        y_sb = keep.tile([P, S + PAD], F32, name="y_sb")
+        t1 = keep.tile([P, T], F32, name="t1")
+        t2 = keep.tile([P, T], F32, name="t2")
+        o_sb = keep.tile([P, T], F32, name="o_sb")
+        dummy = keep.tile([P, 1], F32, name="dummy")
+        dummy2 = keep.tile([P, 1], F32, name="dummy2")
+
+        nc.vector.memset(s1_raw[:].bitcast(I32), 0)
+        nc.vector.memset(dummy[:], 0.0)
+        nc.vector.memset(x_scales[:].bitcast(I32), 0)
+        nc.vector.memset(s2_sb[:].rearrange("p e h -> p (e h)").bitcast(I32), 0)
+        nc.vector.memset(y_sb[:, S : S + PAD], 0.0)
+
+        x_view = xT.rearrange("(p j) t -> p j t", j=4)
+        s1_i32 = w1_scales.rearrange("e s q h -> (e s) q h").bitcast(I32)
+        s2_i32 = w2_scales.rearrange("e s q h -> q (e s) h").bitcast(I32)
+        nc.scalar.activation(out=dummy2[:], in_=dummy[:], func=ACT.Gelu_apprx_tanh)
+
+        w1_i32 = w1_words.rearrange("e s p b -> p (e s) b").bitcast(I32)
+        nc.sync.dma_start(out=w1_raw[:, 0:1, :].bitcast(I32), in_=w1_i32[:, 0:1, :])
+        for q in range(4):
+            nc.sync.dma_start(out=s1_raw[32 * q : 32 * q + 16, :].bitcast(I32), in_=s1_i32[:, 4 * q : 4 * q + 4, :])
+        nc.sync.dma_start(out=w1_raw[:, 1:3, :].bitcast(I32), in_=w1_i32[:, 1:3, :])
+        for lo, hi in ((0, 512), (512, 768)):
+            nc.sync.dma_start(out=x_raw[:, :, lo:hi], in_=x_view[:, :, lo:hi])
+        nc.sync.dma_start(offs_sb[:], offs)
+        nc.sync.dma_start(out=w1_raw[:, 3:4, :].bitcast(I32), in_=w1_i32[:, 3:4, :])
+
+        nc.vector.tensor_copy(
+            out=s1_perm[:].rearrange("p (t m) -> p t m", t=4),
+            in_=s1_raw[:].rearrange("p (m t) -> p t m", t=4),
+        )
+        for e in range(1, E):
+            rows = P - 4 * e
+            nc.sync.dma_start(out=s1_planes[e][0:rows, :].bitcast(I32), in_=s1_perm[4 * e : P, :].bitcast(I32))
+        nc.sync.dma_start(out=w2_sb[:].bitcast(I32), in_=w2_words.rearrange("e s p b -> p (e s) b").bitcast(I32))
+        for q in range(4):
+            nc.sync.dma_start(out=s2_sb[32 * q : 32 * q + 4, :, :].bitcast(I32), in_=s2_i32[4 * q : 4 * q + 4, :, :])
+        nc.sync.dma_start(pos1_sb[:], pos1)
+        nc.sync.dma_start(pos2_sb[:], pos2)
+        for r in range(2):
+            nc.sync.dma_start(out=gate_sb[:, r, :], in_=gate[r])
+
+        def permute(lo, hi):
+            nc.vector.tensor_copy(
+                out=w1_perm[:, lo:hi, :].rearrange("p e b -> p (e b)").bitcast(U16).rearrange("p (e t m) -> p e t m", e=hi - lo, t=4),
+                in_=w1_raw[:, lo:hi, :].rearrange("p e b -> p (e b)").bitcast(U16).rearrange("p (e m t) -> p e t m", e=hi - lo, t=4),
+            )
+
+        def cast(engine, lo, hi):
+            dst = x_bf[:, lo:hi, :].rearrange("p (c i) j -> p c j i", i=4)
+            src = x_raw[:, :, lo:hi].rearrange("p j (c i) -> p c j i", i=4)
+            if engine == "scalar":
+                nc.scalar.copy(out=dst, in_=src)
+            else:
+                nc.vector.tensor_copy(out=dst, in_=src)
+
+        def quantize_x(lo, hi):
+            nc.vector.quantize_mx(
+                out=x_codes[:, lo:hi].bitcast(FP8X4),
+                scales=x_scales[:, lo:hi],
+                in_=x_bf[:, lo:hi, :].rearrange("p t j -> p (t j)"),
+            )
+
+        permute(0, 1)
+        permute(1, 3)
+        cast("vector", 0, 256)
+        cast("scalar", 256, 512)
+        quantize_x(0, 256)
+        cast("vector", 512, 672)
+        cast("scalar", 672, 768)
+        quantize_x(256, 512)
+        quantize_x(512, 768)
+
+        g_codes = [keep.tile([P, C], U32, name="g_codes%d" % e, align_bytes=64) for e in range(E)]
+        g_scales = [keep.tile([P, C], U8, name="g_scales%d" % e, align_bytes=64) for e in range(E)]
+
+        def gather(e, lo, hi):
+            lst = offs_sb[:, (e * C + lo) // 16 : (e * C + hi) // 16]
+            nc.vector.tensor_copy(g_codes[e][:, lo:hi], x_codes[:].indirect(lst))
+            nc.vector.tensor_copy(g_scales[e][:, lo:hi], x_scales[:].indirect(lst))
+
+        y_place = ((0, 0), (1, 0), (1, C), (0, C))
+        y_banks = [ypsum.tile([P, 2 * C], F32, name="y_bank%d" % b) for b in range(2)]
+
+        h = [keep.tile([P, C, 4], BF16, name="h%d" % e, align_bytes=64) for e in range(E)]
+        h_codes = [keep.tile([P, C], U32, name="h_codes%d" % e, align_bytes=64) for e in range(E)]
+        h_scales = [keep.tile([P, C], U8, name="h_scales%d" % e, align_bytes=64) for e in range(E)]
+
+        def first_layer(e):
+            for u in range(2):
+                bank = apsum.tile([P, 4 * U], F32, name="bank")
+                cols = slice(u * U, (u + 1) * U)
+                for t in range(4):
+                    nc.tensor.matmul_mx(
+                        out=bank[:, t * U : (t + 1) * U],
+                        lhsT=w1_perm[:, e, t * 256 : (t + 1) * 256].bitcast(FP4X4),
+                        lhsT_scale=s1_planes[e][:, t * 128 : (t + 1) * 128],
+                        rhs=g_codes[e][:, cols].bitcast(FP8X4),
+                        rhs_scale=g_scales[e][:, cols],
+                        start=True,
+                        stop=True,
+                    )
+                nc.scalar.activation(out=h[e][:, cols, :], in_=bank[:].rearrange("p (t c) -> p c t", t=4), func=ACT.Gelu_apprx_tanh)
+
+        def second_layer(e, lo, hi):
+            nc.vector.quantize_mx(
+                out=h_codes[e][:, lo:hi].bitcast(FP8X4),
+                scales=h_scales[e][:, lo:hi],
+                in_=h[e][:, lo:hi, :].rearrange("p c t -> p (c t)"),
+            )
+            bank, base = y_place[e]
+            nc.tensor.matmul_mx(
+                out=y_banks[bank][:, base + lo : base + hi],
+                lhsT=w2_sb[:, e, :].bitcast(FP4X4),
+                lhsT_scale=s2_sb[:, e, :],
+                rhs=h_codes[e][:, lo:hi].bitcast(FP8X4),
+                rhs_scale=h_scales[e][:, lo:hi],
+                start=True,
+                stop=True,
+            )
+
+        gather(0, 0, U)
+        gather(0, U, C)
+        first_layer(0)
+        gather(1, 0, C)
+        first_layer(1)
+        second_layer(0, 0, C)
+        nc.scalar.copy(out=y_sb[:, 0:C], in_=y_banks[0][:, 0:C])
+        permute(3, 4)
+        gather(2, 0, C)
+        first_layer(2)
+        gather(3, 0, U)
+        gather(3, U, C)
+        first_layer(3)
+        second_layer(1, 0, C)
+        second_layer(2, 0, C)
+        second_layer(3, 0, U)
+        nc.scalar.copy(out=y_sb[:, C : 3 * C], in_=y_banks[1][:])
+        second_layer(3, U, C)
+        nc.vector.tensor_copy(out=y_sb[:, 3 * C : 4 * C], in_=y_banks[0][:, C : 2 * C])
+
+        def pick(lo, hi, p_sb, r, t):
+            nc.vector.tensor_tensor(t[:, lo:hi], y_sb[:].indirect(p_sb[:, lo // 16 : hi // 16]), gate_sb[:, r, lo:hi], ALU.mult)
+
+        def finish(lo, hi):
+            nc.vector.tensor_add(o_sb[:, lo:hi], t1[:, lo:hi], t2[:, lo:hi])
+            nc.sync.dma_start(out=out[:, lo:hi], in_=o_sb[:, lo:hi])
+
+        pick(0, 768, pos1_sb, 0, t1)
+        pick(0, 512, pos2_sb, 1, t2)
+        pick(512, 768, pos2_sb, 1, t2)
+        finish(0, 512)
+        finish(512, 768)

@@ -26,7 +26,7 @@ def tile_moe_cap2_mlp_gelu_kernel(tc, xT, w1_words, w1_scales, w2_words, w2_scal
     nc = tc.nc
     with ExitStack() as ctx:
         keep = ctx.enter_context(tc.tile_pool(name="keep", bufs=1))
-        apsum = ctx.enter_context(tc.psum_pool(name="apsum", bufs=6))
+        apsum = ctx.enter_context(tc.psum_pool(name="apsum", bufs=5))
         ypsum = ctx.enter_context(tc.psum_pool(name="ypsum", bufs=1))
 
         offs_sb = keep.tile([P, S // 16], U16, name="offs_sb")
@@ -126,8 +126,8 @@ def tile_moe_cap2_mlp_gelu_kernel(tc, xT, w1_words, w1_scales, w2_words, w2_scal
             nc.vector.tensor_copy(g_codes[e][:, lo:hi], x_codes[:].indirect(lst))
             nc.vector.tensor_copy(g_scales[e][:, lo:hi], x_scales[:].indirect(lst))
 
-        y_place = ((0, 0), (1, 0), (1, C), (0, C))
-        y_banks = [ypsum.tile([P, 2 * C], F32, name="y_bank%d" % b) for b in range(2)]
+        y_place = {(0, 0): (0, 0), (1, 0): (0, C), (2, 0): (1, 0), (3, 0): (1, C), (3, U): (2, 0)}
+        y_banks = [ypsum.tile([P, 2 * C], F32, name="y_bank%d" % b) for b in range(3)]
 
         h = [keep.tile([P, C, 4], BF16, name="h%d" % e, align_bytes=64) for e in range(E)]
         h_codes = [keep.tile([P, C], U32, name="h_codes%d" % e, align_bytes=64) for e in range(E)]
@@ -155,9 +155,9 @@ def tile_moe_cap2_mlp_gelu_kernel(tc, xT, w1_words, w1_scales, w2_words, w2_scal
                 scales=h_scales[e][:, lo:hi],
                 in_=h[e][:, lo:hi, :].rearrange("p c t -> p (c t)"),
             )
-            bank, base = y_place[e]
+            bank, base = y_place[(e, lo)]
             nc.tensor.matmul_mx(
-                out=y_banks[bank][:, base + lo : base + hi],
+                out=y_banks[bank][:, base : base + hi - lo],
                 lhsT=w2_sb[:, e, :].bitcast(FP4X4),
                 lhsT_scale=s2_sb[:, e, :],
                 rhs=h_codes[e][:, lo:hi].bitcast(FP8X4),
@@ -166,25 +166,27 @@ def tile_moe_cap2_mlp_gelu_kernel(tc, xT, w1_words, w1_scales, w2_words, w2_scal
                 stop=True,
             )
 
+        permute(3, 4)
         gather(0, 0, U)
         gather(0, U, C)
         first_layer(0)
-        gather(1, 0, C)
+        gather(1, 0, U)
+        gather(1, U, C)
         first_layer(1)
-        second_layer(0, 0, C)
-        nc.scalar.copy(out=y_sb[:, 0:C], in_=y_banks[0][:, 0:C])
-        permute(3, 4)
-        gather(2, 0, C)
+        gather(2, 0, U)
+        gather(2, U, C)
         first_layer(2)
         gather(3, 0, U)
         gather(3, U, C)
         first_layer(3)
+        second_layer(0, 0, C)
         second_layer(1, 0, C)
         second_layer(2, 0, C)
         second_layer(3, 0, U)
-        nc.scalar.copy(out=y_sb[:, C : 3 * C], in_=y_banks[1][:])
         second_layer(3, U, C)
-        nc.vector.tensor_copy(out=y_sb[:, 3 * C : 4 * C], in_=y_banks[0][:, C : 2 * C])
+        nc.scalar.copy(out=y_sb[:, 0 : 2 * C], in_=y_banks[0][:])
+        nc.vector.tensor_copy(out=y_sb[:, 2 * C : 3 * C + U], in_=y_banks[1][:, 0 : C + U])
+        nc.scalar.copy(out=y_sb[:, 3 * C + U : S], in_=y_banks[2][:, 0:U])
 
         def pick(lo, hi, p_sb, r, t):
             nc.vector.tensor_tensor(t[:, lo:hi], y_sb[:].indirect(p_sb[:, lo // 16 : hi // 16]), gate_sb[:, r, lo:hi], ALU.mult)
@@ -193,8 +195,11 @@ def tile_moe_cap2_mlp_gelu_kernel(tc, xT, w1_words, w1_scales, w2_words, w2_scal
             nc.vector.tensor_add(o_sb[:, lo:hi], t1[:, lo:hi], t2[:, lo:hi])
             nc.sync.dma_start(out=out[:, lo:hi], in_=o_sb[:, lo:hi])
 
-        pick(0, 768, pos1_sb, 0, t1)
+        pick(0, 512, pos1_sb, 0, t1)
         pick(0, 512, pos2_sb, 1, t2)
-        pick(512, 768, pos2_sb, 1, t2)
+        pick(512, 768, pos1_sb, 0, t1)
         finish(0, 512)
-        finish(512, 768)
+        pick(512, 640, pos2_sb, 1, t2)
+        pick(640, 768, pos2_sb, 1, t2)
+        finish(512, 640)
+        finish(640, 768)

@@ -66,9 +66,10 @@ def tile_moe_cap2_mlp_gelu_kernel(tc, xT, w1_words, w1_scales, w2_words, w2_scal
         nc.sync.dma_start(out=w1_raw[:, 0:1, :].bitcast(I32), in_=w1_i32[:, 0:1, :])
         for q in range(4):
             nc.sync.dma_start(out=s1_raw[32 * q : 32 * q + 16, :].bitcast(I32), in_=s1_i32[:, 4 * q : 4 * q + 4, :])
-        nc.sync.dma_start(out=w1_raw[:, 1:3, :].bitcast(I32), in_=w1_i32[:, 1:3, :])
+        nc.sync.dma_start(out=w1_raw[:, 1:2, :].bitcast(I32), in_=w1_i32[:, 1:2, :])
         for lo, hi in ((0, 512), (512, 768)):
             nc.sync.dma_start(out=x_raw[:, :, lo:hi], in_=x_view[:, :, lo:hi])
+        nc.sync.dma_start(out=w1_raw[:, 2:3, :].bitcast(I32), in_=w1_i32[:, 2:3, :])
         nc.sync.dma_start(offs_sb[:], offs)
         nc.sync.dma_start(out=w1_raw[:, 3:4, :].bitcast(I32), in_=w1_i32[:, 3:4, :])
 
@@ -109,13 +110,15 @@ def tile_moe_cap2_mlp_gelu_kernel(tc, xT, w1_words, w1_scales, w2_words, w2_scal
             )
 
         permute(0, 1)
-        permute(1, 3)
+        permute(1, 2)
         cast("vector", 0, 256)
-        cast("scalar", 256, 512)
+        cast("vector", 256, 288)
+        cast("scalar", 288, 512)
         quantize_x(0, 256)
-        cast("vector", 512, 672)
-        cast("scalar", 672, 768)
         quantize_x(256, 512)
+        cast("vector", 512, 640)
+        cast("scalar", 640, 768)
+        permute(2, 3)
         quantize_x(512, 768)
 
         g_codes = [keep.tile([P, C], U32, name="g_codes%d" % e, align_bytes=64) for e in range(E)]

@@ -51,7 +51,7 @@ def tile_moe_cap2_mlp_gelu_kernel(tc, xT, w1_words, w1_scales, w2_words, w2_scal
         dummy = keep.tile([P, 1], F32, name="dummy")
         dummy2 = keep.tile([P, 1], F32, name="dummy2")
 
-        nc.vector.memset(s1_raw[:].bitcast(I32), 0)
+        nc.gpsimd.memset(s1_raw[:].bitcast(I32), 0)
         nc.vector.memset(dummy[:], 0.0)
         nc.vector.memset(x_scales[:].bitcast(I32), 0)
         nc.vector.memset(s2_sb[:].rearrange("p e h -> p (e h)").bitcast(I32), 0)
@@ -63,10 +63,9 @@ def tile_moe_cap2_mlp_gelu_kernel(tc, xT, w1_words, w1_scales, w2_words, w2_scal
         nc.scalar.activation(out=dummy2[:], in_=dummy[:], func=ACT.Gelu_apprx_tanh)
 
         w1_i32 = w1_words.rearrange("e s p b -> p (e s) b").bitcast(I32)
-        nc.sync.dma_start(out=w1_raw[:, 0:1, :].bitcast(I32), in_=w1_i32[:, 0:1, :])
+        nc.sync.dma_start(out=w1_raw[:, 0:2, :].bitcast(I32), in_=w1_i32[:, 0:2, :])
         for q in range(4):
             nc.sync.dma_start(out=s1_raw[32 * q : 32 * q + 16, :].bitcast(I32), in_=s1_i32[:, 4 * q : 4 * q + 4, :])
-        nc.sync.dma_start(out=w1_raw[:, 1:2, :].bitcast(I32), in_=w1_i32[:, 1:2, :])
         for lo, hi in ((0, 512), (512, 768)):
             nc.sync.dma_start(out=x_raw[:, :, lo:hi], in_=x_view[:, :, lo:hi])
         nc.sync.dma_start(out=w1_raw[:, 2:3, :].bitcast(I32), in_=w1_i32[:, 2:3, :])
@@ -109,8 +108,7 @@ def tile_moe_cap2_mlp_gelu_kernel(tc, xT, w1_words, w1_scales, w2_words, w2_scal
                 in_=x_bf[:, lo:hi, :].rearrange("p t j -> p (t j)"),
             )
 
-        permute(0, 1)
-        permute(1, 2)
+        permute(0, 2)
         cast("vector", 0, 256)
         cast("vector", 256, 288)
         cast("scalar", 288, 512)

@@ -26,8 +26,7 @@ def tile_moe_cap2_mlp_gelu_kernel(tc, xT, w1_words, w1_scales, w2_words, w2_scal
     nc = tc.nc
     with ExitStack() as ctx:
         keep = ctx.enter_context(tc.tile_pool(name="keep", bufs=1))
-        apsum = ctx.enter_context(tc.psum_pool(name="apsum", bufs=5))
-        ypsum = ctx.enter_context(tc.psum_pool(name="ypsum", bufs=1))
+        apsum = ctx.enter_context(tc.psum_pool(name="apsum", bufs=8))
 
         offs_sb = keep.tile([P, S // 16], U16, name="offs_sb")
         pos1_sb = keep.tile([P, T // 16], U16, name="pos1_sb")
@@ -84,8 +83,7 @@ def tile_moe_cap2_mlp_gelu_kernel(tc, xT, w1_words, w1_scales, w2_words, w2_scal
             nc.sync.dma_start(out=s2_sb[32 * q : 32 * q + 4, :, :].bitcast(I32), in_=s2_i32[4 * q : 4 * q + 4, :, :])
         nc.sync.dma_start(pos1_sb[:], pos1)
         nc.sync.dma_start(pos2_sb[:], pos2)
-        for r in range(2):
-            nc.sync.dma_start(out=gate_sb[:, r, :], in_=gate[r])
+        nc.sync.dma_start(out=gate_sb[:], in_=gate.rearrange("r p t -> p r t"))
 
         def permute(lo, hi):
             nc.vector.tensor_copy(
@@ -122,13 +120,14 @@ def tile_moe_cap2_mlp_gelu_kernel(tc, xT, w1_words, w1_scales, w2_words, w2_scal
         g_codes = [keep.tile([P, C], U32, name="g_codes%d" % e, align_bytes=64) for e in range(E)]
         g_scales = [keep.tile([P, C], U8, name="g_scales%d" % e, align_bytes=64) for e in range(E)]
 
-        def gather(e, lo, hi):
-            lst = offs_sb[:, (e * C + lo) // 16 : (e * C + hi) // 16]
-            nc.vector.tensor_copy(g_codes[e][:, lo:hi], x_codes[:].indirect(lst))
-            nc.vector.tensor_copy(g_scales[e][:, lo:hi], x_scales[:].indirect(lst))
+        def gather(e, scale_width, code_width):
+            for lo in range(0, C, U):
+                for dst, src, width in ((g_scales[e], x_scales, scale_width), (g_codes[e], x_codes, code_width)):
+                    if lo % width == 0:
+                        lst = offs_sb[:, (e * C + lo) // 16 : (e * C + lo + width) // 16]
+                        nc.vector.tensor_copy(dst[:, lo : lo + width], src[:].indirect(lst))
 
         y_place = {(0, 0): (0, 0), (1, 0): (0, C), (2, 0): (1, 0), (3, 0): (1, C), (3, U): (2, 0)}
-        y_banks = [ypsum.tile([P, 2 * C], F32, name="y_bank%d" % b) for b in range(3)]
 
         h = [keep.tile([P, C, 4], BF16, name="h%d" % e, align_bytes=64) for e in range(E)]
         h_codes = [keep.tile([P, C], U32, name="h_codes%d" % e, align_bytes=64) for e in range(E)]
@@ -168,18 +167,15 @@ def tile_moe_cap2_mlp_gelu_kernel(tc, xT, w1_words, w1_scales, w2_words, w2_scal
             )
 
         permute(3, 4)
-        gather(0, 0, U)
-        gather(0, U, C)
+        gather(0, C, C)
         first_layer(0)
-        gather(1, 0, U)
-        gather(1, U, C)
+        gather(1, C, C)
         first_layer(1)
-        gather(2, 0, U)
-        gather(2, U, C)
+        gather(2, C, U)
         first_layer(2)
-        gather(3, 0, U)
-        gather(3, U, C)
+        gather(3, U, U)
         first_layer(3)
+        y_banks = [apsum.tile([P, 4 * U], F32, name="bank") for b in range(3)]
         second_layer(0, 0, C)
         second_layer(1, 0, C)
         second_layer(2, 0, C)

@@ -117,15 +117,11 @@ def tile_moe_cap2_mlp_gelu_kernel(tc, xT, w1_words, w1_scales, w2_words, w2_scal
         permute(2, 3)
         quantize_x(512, 768)
 
-        g_codes = [keep.tile([P, C], U32, name="g_codes%d" % e, align_bytes=64) for e in range(E)]
-        g_scales = [keep.tile([P, C], U8, name="g_scales%d" % e, align_bytes=64) for e in range(E)]
+        g_codes = keep.tile([P, S], U32, name="g_codes", align_bytes=64)
+        g_scales = keep.tile([P, S], U8, name="g_scales", align_bytes=64)
 
-        def gather(e, scale_width, code_width):
-            for lo in range(0, C, U):
-                for dst, src, width in ((g_scales[e], x_scales, scale_width), (g_codes[e], x_codes, code_width)):
-                    if lo % width == 0:
-                        lst = offs_sb[:, (e * C + lo) // 16 : (e * C + lo + width) // 16]
-                        nc.vector.tensor_copy(dst[:, lo : lo + width], src[:].indirect(lst))
+        def gather(dst, src, lo, hi):
+            nc.vector.tensor_copy(dst[:, lo:hi], src[:].indirect(offs_sb[:, lo // 16 : hi // 16]))
 
         y_place = {(0, 0): (0, 0), (1, 0): (0, C), (2, 0): (1, 0), (3, 0): (1, C), (3, U): (2, 0)}
 
@@ -133,21 +129,21 @@ def tile_moe_cap2_mlp_gelu_kernel(tc, xT, w1_words, w1_scales, w2_words, w2_scal
         h_codes = [keep.tile([P, C], U32, name="h_codes%d" % e, align_bytes=64) for e in range(E)]
         h_scales = [keep.tile([P, C], U8, name="h_scales%d" % e, align_bytes=64) for e in range(E)]
 
-        def first_layer(e):
-            for u in range(2):
-                bank = apsum.tile([P, 4 * U], F32, name="bank")
-                cols = slice(u * U, (u + 1) * U)
-                for t in range(4):
-                    nc.tensor.matmul_mx(
-                        out=bank[:, t * U : (t + 1) * U],
-                        lhsT=w1_perm[:, e, t * 256 : (t + 1) * 256].bitcast(FP4X4),
-                        lhsT_scale=s1_planes[e][:, t * 128 : (t + 1) * 128],
-                        rhs=g_codes[e][:, cols].bitcast(FP8X4),
-                        rhs_scale=g_scales[e][:, cols],
-                        start=True,
-                        stop=True,
-                    )
-                nc.scalar.activation(out=h[e][:, cols, :], in_=bank[:].rearrange("p (t c) -> p c t", t=4), func=ACT.Gelu_apprx_tanh)
+        def first_layer(unit):
+            e, u = divmod(unit, 2)
+            bank = apsum.tile([P, 4 * U], F32, name="bank")
+            slots = slice(unit * U, (unit + 1) * U)
+            for t in range(4):
+                nc.tensor.matmul_mx(
+                    out=bank[:, t * U : (t + 1) * U],
+                    lhsT=w1_perm[:, e, t * 256 : (t + 1) * 256].bitcast(FP4X4),
+                    lhsT_scale=s1_planes[e][:, t * 128 : (t + 1) * 128],
+                    rhs=g_codes[:, slots].bitcast(FP8X4),
+                    rhs_scale=g_scales[:, slots],
+                    start=True,
+                    stop=True,
+                )
+            nc.scalar.activation(out=h[e][:, u * U : (u + 1) * U, :], in_=bank[:].rearrange("p (t c) -> p c t", t=4), func=ACT.Gelu_apprx_tanh)
 
         def second_layer(e, lo, hi):
             nc.vector.quantize_mx(
@@ -167,14 +163,12 @@ def tile_moe_cap2_mlp_gelu_kernel(tc, xT, w1_words, w1_scales, w2_words, w2_scal
             )
 
         permute(3, 4)
-        gather(0, C, C)
-        first_layer(0)
-        gather(1, C, C)
-        first_layer(1)
-        gather(2, C, U)
-        first_layer(2)
-        gather(3, U, U)
-        first_layer(3)
+        for unit in range(S // U):
+            if unit == 0 or unit % 2 == 1:
+                last = unit if unit in (0, S // U - 1) else unit + 1
+                gather(g_scales, x_scales, unit * U, (last + 1) * U)
+            gather(g_codes, x_codes, unit * U, (unit + 1) * U)
+            first_layer(unit)
         y_banks = [apsum.tile([P, 4 * U], F32, name="bank") for b in range(3)]
         second_layer(0, 0, C)
         second_layer(1, 0, C)

@@ -107,9 +107,10 @@ def tile_moe_cap2_mlp_gelu_kernel(tc, xT, w1_words, w1_scales, w2_words, w2_scal
             )
 
         permute(0, 2)
-        cast("vector", 0, 256)
-        cast("vector", 256, 288)
-        cast("scalar", 288, 512)
+        cast("vector", 0, 160)
+        cast("scalar", 160, 256)
+        cast("vector", 256, 352)
+        cast("scalar", 352, 512)
         quantize_x(0, 256)
         quantize_x(256, 512)
         cast("vector", 512, 640)
@@ -189,8 +190,7 @@ def tile_moe_cap2_mlp_gelu_kernel(tc, xT, w1_words, w1_scales, w2_words, w2_scal
         pick(0, 512, pos1_sb, 0, t1)
         pick(0, 512, pos2_sb, 1, t2)
         pick(512, 768, pos1_sb, 0, t1)
-        finish(0, 512)
-        pick(512, 640, pos2_sb, 1, t2)
-        pick(640, 768, pos2_sb, 1, t2)
-        finish(512, 640)
-        finish(640, 768)
+        finish(0, 320)
+        pick(512, 768, pos2_sb, 1, t2)
+        finish(320, 512)
+        finish(512, 768)

@@ -7,6 +7,14 @@ PAD = 32
 S = E * C
 P = 128
 U = 128
+UNITS = S // U
+LIST = 16
+
+X_FIRST = 512
+X_BLOCK = 256
+VECTOR_SHARE = (160, 96, 128)
+OUT_FIRST = 576
+OUT_EARLY = 384
 
 F32 = mybir.dt.float32
 BF16 = mybir.dt.bfloat16
@@ -26,11 +34,11 @@ def tile_moe_cap2_mlp_gelu_kernel(tc, xT, w1_words, w1_scales, w2_words, w2_scal
     nc = tc.nc
     with ExitStack() as ctx:
         keep = ctx.enter_context(tc.tile_pool(name="keep", bufs=1))
-        apsum = ctx.enter_context(tc.psum_pool(name="apsum", bufs=8))
+        psum = ctx.enter_context(tc.psum_pool(name="psum", bufs=UNITS))
 
-        offs_sb = keep.tile([P, S // 16], U16, name="offs_sb")
-        pos1_sb = keep.tile([P, T // 16], U16, name="pos1_sb")
-        pos2_sb = keep.tile([P, T // 16], U16, name="pos2_sb")
+        offs_sb = keep.tile([P, S // LIST], U16, name="offs_sb")
+        pos1_sb = keep.tile([P, T // LIST], U16, name="pos1_sb")
+        pos2_sb = keep.tile([P, T // LIST], U16, name="pos2_sb")
         x_raw = keep.tile([P, 4, T], F32, name="x_raw")
         x_bf = keep.tile([P, T, 4], BF16, name="x_bf", align_bytes=64)
         x_codes = keep.tile([P, T], U32, name="x_codes", align_bytes=64)
@@ -41,156 +49,154 @@ def tile_moe_cap2_mlp_gelu_kernel(tc, xT, w1_words, w1_scales, w2_words, w2_scal
         s1_perm = keep.tile([P, H], U8, name="s1_perm", align_bytes=64)
         s1_planes = [s1_perm] + [keep.tile([P, H], U8, name="s1_plane%d" % e, align_bytes=64) for e in range(1, E)]
         w2_sb = keep.tile([P, E, 2 * N], U8, name="w2_sb", align_bytes=64)
-        s2_sb = keep.tile([P, E, N], U8, name="s2_sb", align_bytes=64)
+        s2_planes = keep.tile([P, E, N], U8, name="s2_planes", align_bytes=64)
         gate_sb = keep.tile([P, 2, T], F32, name="gate_sb")
         y_sb = keep.tile([P, S + PAD], F32, name="y_sb")
-        t1 = keep.tile([P, T], F32, name="t1")
-        t2 = keep.tile([P, T], F32, name="t2")
-        o_sb = keep.tile([P, T], F32, name="o_sb")
-        dummy = keep.tile([P, 1], F32, name="dummy")
-        dummy2 = keep.tile([P, 1], F32, name="dummy2")
+        first_sb = keep.tile([P, T], F32, name="first_sb")
+        second_sb = keep.tile([P, T], F32, name="second_sb")
+        out_sb = keep.tile([P, T], F32, name="out_sb")
+        zeros = keep.tile([P, PAD], F32, name="zeros")
 
         nc.gpsimd.memset(s1_raw[:].bitcast(I32), 0)
-        nc.vector.memset(dummy[:], 0.0)
+        nc.vector.memset(zeros[:], 0.0)
         nc.vector.memset(x_scales[:].bitcast(I32), 0)
-        nc.vector.memset(s2_sb[:].rearrange("p e h -> p (e h)").bitcast(I32), 0)
-        nc.vector.memset(y_sb[:, S : S + PAD], 0.0)
+        nc.vector.memset(s2_planes[:].rearrange("p e n -> p (e n)").bitcast(I32), 0)
+
+        nc.scalar.activation(out=y_sb[:, S : S + PAD], in_=zeros[:], func=ACT.Gelu_apprx_tanh)
 
         x_view = xT.rearrange("(p j) t -> p j t", j=4)
-        s1_i32 = w1_scales.rearrange("e s q h -> (e s) q h").bitcast(I32)
-        s2_i32 = w2_scales.rearrange("e s q h -> q (e s) h").bitcast(I32)
-        nc.scalar.activation(out=dummy2[:], in_=dummy[:], func=ACT.Gelu_apprx_tanh)
-
         w1_i32 = w1_words.rearrange("e s p b -> p (e s) b").bitcast(I32)
-        nc.sync.dma_start(out=w1_raw[:, 0:2, :].bitcast(I32), in_=w1_i32[:, 0:2, :])
+        s1_i32 = w1_scales.rearrange("e s g h -> (e s) g h").bitcast(I32)
+        s2_i32 = w2_scales.rearrange("e s g n -> g (e s) n").bitcast(I32)
+
+        def load_w1(lo, hi):
+            nc.sync.dma_start(out=w1_raw[:, lo:hi, :].bitcast(I32), in_=w1_i32[:, lo:hi, :])
+
+        load_w1(0, 2)
         for q in range(4):
-            nc.sync.dma_start(out=s1_raw[32 * q : 32 * q + 16, :].bitcast(I32), in_=s1_i32[:, 4 * q : 4 * q + 4, :])
-        for lo, hi in ((0, 512), (512, 768)):
+            nc.sync.dma_start(out=s1_raw[32 * q : 32 * q + 4 * E, :].bitcast(I32), in_=s1_i32[:, 4 * q : 4 * q + 4, :])
+        for lo, hi in ((0, X_FIRST), (X_FIRST, T)):
             nc.sync.dma_start(out=x_raw[:, :, lo:hi], in_=x_view[:, :, lo:hi])
-        nc.sync.dma_start(out=w1_raw[:, 2:3, :].bitcast(I32), in_=w1_i32[:, 2:3, :])
+        load_w1(2, 3)
         nc.sync.dma_start(offs_sb[:], offs)
-        nc.sync.dma_start(out=w1_raw[:, 3:4, :].bitcast(I32), in_=w1_i32[:, 3:4, :])
+        load_w1(3, 4)
 
         nc.vector.tensor_copy(
             out=s1_perm[:].rearrange("p (t m) -> p t m", t=4),
             in_=s1_raw[:].rearrange("p (m t) -> p t m", t=4),
         )
         for e in range(1, E):
-            rows = P - 4 * e
-            nc.sync.dma_start(out=s1_planes[e][0:rows, :].bitcast(I32), in_=s1_perm[4 * e : P, :].bitcast(I32))
+            nc.sync.dma_start(out=s1_planes[e][0 : P - 4 * e, :].bitcast(I32), in_=s1_perm[4 * e : P, :].bitcast(I32))
         nc.sync.dma_start(out=w2_sb[:].bitcast(I32), in_=w2_words.rearrange("e s p b -> p (e s) b").bitcast(I32))
         for q in range(4):
-            nc.sync.dma_start(out=s2_sb[32 * q : 32 * q + 4, :, :].bitcast(I32), in_=s2_i32[4 * q : 4 * q + 4, :, :])
+            nc.sync.dma_start(out=s2_planes[32 * q : 32 * q + 4, :, :].bitcast(I32), in_=s2_i32[4 * q : 4 * q + 4, :, :])
         nc.sync.dma_start(pos1_sb[:], pos1)
         nc.sync.dma_start(pos2_sb[:], pos2)
         nc.sync.dma_start(out=gate_sb[:], in_=gate.rearrange("r p t -> p r t"))
 
-        def permute(lo, hi):
+        def reorder_w1(lo, hi):
             nc.vector.tensor_copy(
                 out=w1_perm[:, lo:hi, :].rearrange("p e b -> p (e b)").bitcast(U16).rearrange("p (e t m) -> p e t m", e=hi - lo, t=4),
                 in_=w1_raw[:, lo:hi, :].rearrange("p e b -> p (e b)").bitcast(U16).rearrange("p (e m t) -> p e t m", e=hi - lo, t=4),
             )
 
-        def cast(engine, lo, hi):
-            dst = x_bf[:, lo:hi, :].rearrange("p (c i) j -> p c j i", i=4)
-            src = x_raw[:, :, lo:hi].rearrange("p j (c i) -> p c j i", i=4)
-            if engine == "scalar":
-                nc.scalar.copy(out=dst, in_=src)
-            else:
-                nc.vector.tensor_copy(out=dst, in_=src)
+        def round_block(block):
+            lo = block * X_BLOCK
+            cut = lo + VECTOR_SHARE[block]
+            for copy, a, b in ((nc.vector.tensor_copy, lo, cut), (nc.scalar.copy, cut, lo + X_BLOCK)):
+                copy(
+                    out=x_bf[:, a:b, :].rearrange("p (c i) j -> p c j i", i=4),
+                    in_=x_raw[:, :, a:b].rearrange("p j (c i) -> p c j i", i=4),
+                )
 
-        def quantize_x(lo, hi):
+        def quantize_block(block):
+            tokens = slice(block * X_BLOCK, (block + 1) * X_BLOCK)
             nc.vector.quantize_mx(
-                out=x_codes[:, lo:hi].bitcast(FP8X4),
-                scales=x_scales[:, lo:hi],
-                in_=x_bf[:, lo:hi, :].rearrange("p t j -> p (t j)"),
+                out=x_codes[:, tokens].bitcast(FP8X4),
+                scales=x_scales[:, tokens],
+                in_=x_bf[:, tokens, :].rearrange("p t j -> p (t j)"),
             )
 
-        permute(0, 2)
-        cast("vector", 0, 160)
-        cast("scalar", 160, 256)
-        cast("vector", 256, 352)
-        cast("scalar", 352, 512)
-        quantize_x(0, 256)
-        quantize_x(256, 512)
-        cast("vector", 512, 640)
-        cast("scalar", 640, 768)
-        permute(2, 3)
-        quantize_x(512, 768)
+        reorder_w1(0, 2)
+        round_block(0)
+        round_block(1)
+        quantize_block(0)
+        quantize_block(1)
+        round_block(2)
+        reorder_w1(2, 3)
+        quantize_block(2)
 
         g_codes = keep.tile([P, S], U32, name="g_codes", align_bytes=64)
         g_scales = keep.tile([P, S], U8, name="g_scales", align_bytes=64)
-
-        def gather(dst, src, lo, hi):
-            nc.vector.tensor_copy(dst[:, lo:hi], src[:].indirect(offs_sb[:, lo // 16 : hi // 16]))
-
-        y_place = {(0, 0): (0, 0), (1, 0): (0, C), (2, 0): (1, 0), (3, 0): (1, C), (3, U): (2, 0)}
-
         h = [keep.tile([P, C, 4], BF16, name="h%d" % e, align_bytes=64) for e in range(E)]
         h_codes = [keep.tile([P, C], U32, name="h_codes%d" % e, align_bytes=64) for e in range(E)]
         h_scales = [keep.tile([P, C], U8, name="h_scales%d" % e, align_bytes=64) for e in range(E)]
 
+        def gather(dst, src, lo, hi):
+            nc.vector.tensor_copy(dst[:, lo:hi], src[:].indirect(offs_sb[:, lo // LIST : hi // LIST]))
+
         def first_layer(unit):
-            e, u = divmod(unit, 2)
-            bank = apsum.tile([P, 4 * U], F32, name="bank")
+            e, half = divmod(unit, 2)
+            bank = psum.tile([P, 4 * U], F32, name="bank")
             slots = slice(unit * U, (unit + 1) * U)
             for t in range(4):
                 nc.tensor.matmul_mx(
                     out=bank[:, t * U : (t + 1) * U],
-                    lhsT=w1_perm[:, e, t * 256 : (t + 1) * 256].bitcast(FP4X4),
-                    lhsT_scale=s1_planes[e][:, t * 128 : (t + 1) * 128],
+                    lhsT=w1_perm[:, e, t * 2 * P : (t + 1) * 2 * P].bitcast(FP4X4),
+                    lhsT_scale=s1_planes[e][:, t * P : (t + 1) * P],
                     rhs=g_codes[:, slots].bitcast(FP8X4),
                     rhs_scale=g_scales[:, slots],
                     start=True,
                     stop=True,
                 )
-            nc.scalar.activation(out=h[e][:, u * U : (u + 1) * U, :], in_=bank[:].rearrange("p (t c) -> p c t", t=4), func=ACT.Gelu_apprx_tanh)
+            nc.scalar.activation(out=h[e][:, half * U : (half + 1) * U, :], in_=bank[:].rearrange("p (t c) -> p c t", t=4), func=ACT.Gelu_apprx_tanh)
 
-        def second_layer(e, lo, hi):
+        def second_layer(e, lo, hi, y_psum):
             nc.vector.quantize_mx(
                 out=h_codes[e][:, lo:hi].bitcast(FP8X4),
                 scales=h_scales[e][:, lo:hi],
                 in_=h[e][:, lo:hi, :].rearrange("p c t -> p (c t)"),
             )
-            bank, base = y_place[(e, lo)]
             nc.tensor.matmul_mx(
-                out=y_banks[bank][:, base : base + hi - lo],
+                out=y_psum,
                 lhsT=w2_sb[:, e, :].bitcast(FP4X4),
-                lhsT_scale=s2_sb[:, e, :],
+                lhsT_scale=s2_planes[:, e, :],
                 rhs=h_codes[e][:, lo:hi].bitcast(FP8X4),
                 rhs_scale=h_scales[e][:, lo:hi],
                 start=True,
                 stop=True,
             )
 
-        permute(3, 4)
-        for unit in range(S // U):
+        reorder_w1(3, 4)
+        for unit in range(UNITS):
             if unit == 0 or unit % 2 == 1:
-                last = unit if unit in (0, S // U - 1) else unit + 1
-                gather(g_scales, x_scales, unit * U, (last + 1) * U)
+                served = 1 if unit in (0, UNITS - 1) else 2
+                gather(g_scales, x_scales, unit * U, (unit + served) * U)
             gather(g_codes, x_codes, unit * U, (unit + 1) * U)
             first_layer(unit)
-        y_banks = [apsum.tile([P, 4 * U], F32, name="bank") for b in range(3)]
-        second_layer(0, 0, C)
-        second_layer(1, 0, C)
-        second_layer(2, 0, C)
-        second_layer(3, 0, U)
-        second_layer(3, U, C)
-        nc.scalar.copy(out=y_sb[:, 0 : 2 * C], in_=y_banks[0][:])
-        nc.vector.tensor_copy(out=y_sb[:, 2 * C : 3 * C + U], in_=y_banks[1][:, 0 : C + U])
-        nc.scalar.copy(out=y_sb[:, 3 * C + U : S], in_=y_banks[2][:, 0:U])
 
-        def pick(lo, hi, p_sb, r, t):
-            nc.vector.tensor_tensor(t[:, lo:hi], y_sb[:].indirect(p_sb[:, lo // 16 : hi // 16]), gate_sb[:, r, lo:hi], ALU.mult)
+        y_banks = [psum.tile([P, 4 * U], F32, name="bank") for b in range(4)]
+        second_layer(0, 0, C, y_banks[0][:, 0:C])
+        second_layer(1, 0, C, y_banks[0][:, C : 2 * C])
+        second_layer(2, 0, C, y_banks[1][:, 0:C])
+        second_layer(3, 0, U, y_banks[2][:, 0:U])
+        second_layer(3, U, C, y_banks[3][:, 0:U])
+        nc.scalar.copy(out=y_sb[:, 0 : 2 * C], in_=y_banks[0][:])
+        nc.vector.tensor_copy(out=y_sb[:, 2 * C : 3 * C], in_=y_banks[1][:, 0:C])
+        nc.scalar.copy(out=y_sb[:, 3 * C : S - U], in_=y_banks[2][:, 0:U])
+        nc.scalar.copy(out=y_sb[:, S - U : S], in_=y_banks[3][:, 0:U])
+
+        def pick(dst, pos_sb, choice, lo, hi):
+            nc.vector.tensor_tensor(dst[:, lo:hi], y_sb[:].indirect(pos_sb[:, lo // LIST : hi // LIST]), gate_sb[:, choice, lo:hi], ALU.mult)
 
         def finish(lo, hi):
-            nc.vector.tensor_add(o_sb[:, lo:hi], t1[:, lo:hi], t2[:, lo:hi])
-            nc.sync.dma_start(out=out[:, lo:hi], in_=o_sb[:, lo:hi])
+            nc.vector.tensor_add(out_sb[:, lo:hi], first_sb[:, lo:hi], second_sb[:, lo:hi])
+            nc.sync.dma_start(out=out[:, lo:hi], in_=out_sb[:, lo:hi])
 
-        pick(0, 512, pos1_sb, 0, t1)
-        pick(0, 512, pos2_sb, 1, t2)
-        pick(512, 768, pos1_sb, 0, t1)
-        finish(0, 320)
-        pick(512, 768, pos2_sb, 1, t2)
-        finish(320, 512)
-        finish(512, 768)
+        pick(first_sb, pos1_sb, 0, 0, OUT_FIRST)
+        pick(second_sb, pos2_sb, 1, 0, OUT_FIRST)
+        pick(first_sb, pos1_sb, 0, OUT_FIRST, T)
+        finish(0, OUT_EARLY)
+        pick(second_sb, pos2_sb, 1, OUT_FIRST, T)
+        finish(OUT_EARLY, OUT_FIRST)
+        finish(OUT_FIRST, T)

@@ -40,11 +40,11 @@ def tile_moe_cap2_mlp_gelu_kernel(tc, xT, w1_words, w1_scales, w2_words, w2_scal
         pos1_sb = keep.tile([P, T // LIST], U16, name="pos1_sb")
         pos2_sb = keep.tile([P, T // LIST], U16, name="pos2_sb")
         x_raw = keep.tile([P, 4, T], F32, name="x_raw")
-        x_bf = keep.tile([P, T, 4], BF16, name="x_bf", align_bytes=64)
+        x_bf = keep.tile([P, T, 4], BF16, name="x_bf", tag="turns", align_bytes=64)
         x_codes = keep.tile([P, T], U32, name="x_codes", align_bytes=64)
         x_scales = keep.tile([P, T], U8, name="x_scales", align_bytes=64)
         w1_raw = keep.tile([P, E, 2 * H], U8, name="w1_raw", align_bytes=64)
-        w1_perm = keep.tile([P, E, 2 * H], U8, name="w1_perm", align_bytes=64)
+        w1_early = keep.tile([P, 2, 2 * H], U8, name="w1_early", align_bytes=64)
         s1_raw = keep.tile([P, H], U8, name="s1_raw", align_bytes=64)
         s1_perm = keep.tile([P, H], U8, name="s1_perm", align_bytes=64)
         s1_planes = [s1_perm] + [keep.tile([P, H], U8, name="s1_plane%d" % e, align_bytes=64) for e in range(1, E)]
@@ -94,9 +94,9 @@ def tile_moe_cap2_mlp_gelu_kernel(tc, xT, w1_words, w1_scales, w2_words, w2_scal
         nc.sync.dma_start(pos2_sb[:], pos2)
         nc.sync.dma_start(out=gate_sb[:], in_=gate.rearrange("r p t -> p r t"))
 
-        def reorder_w1(lo, hi):
-            nc.vector.tensor_copy(
-                out=w1_perm[:, lo:hi, :].rearrange("p e b -> p (e b)").bitcast(U16).rearrange("p (e t m) -> p e t m", e=hi - lo, t=4),
+        def reorder_w1(engine, dst, lo, hi):
+            engine.tensor_copy(
+                out=dst.rearrange("p e b -> p (e b)").bitcast(U16).rearrange("p (e t m) -> p e t m", e=hi - lo, t=4),
                 in_=w1_raw[:, lo:hi, :].rearrange("p e b -> p (e b)").bitcast(U16).rearrange("p (e m t) -> p e t m", e=hi - lo, t=4),
             )
 
@@ -117,14 +117,17 @@ def tile_moe_cap2_mlp_gelu_kernel(tc, xT, w1_words, w1_scales, w2_words, w2_scal
                 in_=x_bf[:, tokens, :].rearrange("p t j -> p (t j)"),
             )
 
-        reorder_w1(0, 2)
+        reorder_w1(nc.vector, w1_early[:], 0, 2)
         round_block(0)
         round_block(1)
         quantize_block(0)
-        quantize_block(1)
         round_block(2)
-        reorder_w1(2, 3)
+        quantize_block(1)
         quantize_block(2)
+        w1_late = keep.tile([P, 2, 2 * H], U8, name="w1_late", tag="turns", align_bytes=64)
+        reorder_w1(nc.gpsimd, w1_late[:, 0:1, :], 2, 3)
+        reorder_w1(nc.gpsimd, w1_late[:, 1:2, :], 3, 4)
+        w1_perm = [w1_early[:, 0, :], w1_early[:, 1, :], w1_late[:, 0, :], w1_late[:, 1, :]]
 
         g_codes = keep.tile([P, S], U32, name="g_codes", align_bytes=64)
         g_scales = keep.tile([P, S], U8, name="g_scales", align_bytes=64)
@@ -142,7 +145,7 @@ def tile_moe_cap2_mlp_gelu_kernel(tc, xT, w1_words, w1_scales, w2_words, w2_scal
             for t in range(4):
                 nc.tensor.matmul_mx(
                     out=bank[:, t * U : (t + 1) * U],
-                    lhsT=w1_perm[:, e, t * 2 * P : (t + 1) * 2 * P].bitcast(FP4X4),
+                    lhsT=w1_perm[e][:, t * 2 * P : (t + 1) * 2 * P].bitcast(FP4X4),
                     lhsT_scale=s1_planes[e][:, t * P : (t + 1) * P],
                     rhs=g_codes[:, slots].bitcast(FP8X4),
                     rhs_scale=g_scales[:, slots],
@@ -167,7 +170,6 @@ def tile_moe_cap2_mlp_gelu_kernel(tc, xT, w1_words, w1_scales, w2_words, w2_scal
                 stop=True,
             )
 
-        reorder_w1(3, 4)
         for unit in range(UNITS):
             if unit == 0 or unit % 2 == 1:
                 served = 1 if unit in (0, UNITS - 1) else 2

@@ -10,11 +10,11 @@ U = 128
 UNITS = S // U
 LIST = 16
 
-X_FIRST = 512
+X_EDGES = (0, 256, 512, 640, 768)
 X_BLOCK = 256
-VECTOR_SHARE = (160, 96, 128)
-OUT_FIRST = 576
-OUT_EARLY = 384
+VECTOR_SHARE = (160, 192, 32, 96)
+OUT_FIRST = 640
+OUT_EARLY = 512
 
 F32 = mybir.dt.float32
 BF16 = mybir.dt.bfloat16
@@ -39,30 +39,24 @@ def tile_moe_cap2_mlp_gelu_kernel(tc, xT, w1_words, w1_scales, w2_words, w2_scal
         offs_sb = keep.tile([P, S // LIST], U16, name="offs_sb")
         pos1_sb = keep.tile([P, T // LIST], U16, name="pos1_sb")
         pos2_sb = keep.tile([P, T // LIST], U16, name="pos2_sb")
-        x_raw = keep.tile([P, 4, T], F32, name="x_raw")
+        x_raw = [keep.tile([P, 4, hi - lo], F32, name="x_raw%d" % b, tag="x%d" % b, align_bytes=64) for b, (lo, hi) in enumerate(zip(X_EDGES, X_EDGES[1:]))]
         x_bf = keep.tile([P, T, 4], BF16, name="x_bf", tag="turns", align_bytes=64)
         x_codes = keep.tile([P, T], U32, name="x_codes", align_bytes=64)
         x_scales = keep.tile([P, T], U8, name="x_scales", align_bytes=64)
         w1_raw = keep.tile([P, E, 2 * H], U8, name="w1_raw", align_bytes=64)
-        w1_early = keep.tile([P, 2, 2 * H], U8, name="w1_early", align_bytes=64)
-        s1_raw = keep.tile([P, H], U8, name="s1_raw", align_bytes=64)
+        s1_rows = keep.tile([P, H // 4], I32, name="s1_rows", align_bytes=64)
+        s1_raw = keep.tile([P, H], U8, name="s1_raw", tag="scale_rows", align_bytes=64)
         s1_perm = keep.tile([P, H], U8, name="s1_perm", align_bytes=64)
         s1_planes = [s1_perm] + [keep.tile([P, H], U8, name="s1_plane%d" % e, align_bytes=64) for e in range(1, E)]
-        w2_sb = keep.tile([P, E, 2 * N], U8, name="w2_sb", align_bytes=64)
-        s2_planes = keep.tile([P, E, N], U8, name="s2_planes", align_bytes=64)
-        gate_sb = keep.tile([P, 2, T], F32, name="gate_sb")
         y_sb = keep.tile([P, S + PAD], F32, name="y_sb")
         first_sb = keep.tile([P, T], F32, name="first_sb")
         second_sb = keep.tile([P, T], F32, name="second_sb")
         out_sb = keep.tile([P, T], F32, name="out_sb")
         zeros = keep.tile([P, PAD], F32, name="zeros")
 
-        nc.gpsimd.memset(s1_raw[:].bitcast(I32), 0)
         nc.vector.memset(zeros[:], 0.0)
+        nc.vector.memset(s1_raw[:].bitcast(I32), 0)
         nc.vector.memset(x_scales[:].bitcast(I32), 0)
-        nc.vector.memset(s2_planes[:].rearrange("p e n -> p (e n)").bitcast(I32), 0)
-
-        nc.scalar.activation(out=y_sb[:, S : S + PAD], in_=zeros[:], func=ACT.Gelu_apprx_tanh)
 
         x_view = xT.rearrange("(p j) t -> p j t", j=4)
         w1_i32 = w1_words.rearrange("e s p b -> p (e s) b").bitcast(I32)
@@ -72,62 +66,70 @@ def tile_moe_cap2_mlp_gelu_kernel(tc, xT, w1_words, w1_scales, w2_words, w2_scal
         def load_w1(lo, hi):
             nc.sync.dma_start(out=w1_raw[:, lo:hi, :].bitcast(I32), in_=w1_i32[:, lo:hi, :])
 
-        load_w1(0, 2)
-        for q in range(4):
-            nc.sync.dma_start(out=s1_raw[32 * q : 32 * q + 4 * E, :].bitcast(I32), in_=s1_i32[:, 4 * q : 4 * q + 4, :])
-        for lo, hi in ((0, X_FIRST), (X_FIRST, T)):
-            nc.sync.dma_start(out=x_raw[:, :, lo:hi], in_=x_view[:, :, lo:hi])
-        load_w1(2, 3)
-        nc.sync.dma_start(offs_sb[:], offs)
-        load_w1(3, 4)
+        def load_x(block):
+            lo, hi = X_EDGES[block], X_EDGES[block + 1]
+            nc.sync.dma_start(out=x_raw[block][:], in_=x_view[:, :, lo:hi])
 
+        for q in range(4):
+            nc.sync.dma_start(out=s1_rows[32 * q : 32 * q + 4 * E, :], in_=s1_i32[:, 4 * q : 4 * q + 4, :])
+        nc.scalar.activation(out=y_sb[:, S : S + PAD], in_=zeros[:], func=ACT.Gelu_apprx_tanh)
+
+        for block in range(4):
+            load_x(block)
+        load_w1(0, 1)
+        nc.sync.dma_start(offs_sb[:], offs)
+        load_w1(1, 4)
+
+        for q in range(4):
+            nc.vector.tensor_copy(out=s1_raw[32 * q : 32 * q + 4 * E, :].bitcast(I32), in_=s1_rows[32 * q : 32 * q + 4 * E, :])
         nc.vector.tensor_copy(
             out=s1_perm[:].rearrange("p (t m) -> p t m", t=4),
             in_=s1_raw[:].rearrange("p (m t) -> p t m", t=4),
         )
         for e in range(1, E):
-            nc.sync.dma_start(out=s1_planes[e][0 : P - 4 * e, :].bitcast(I32), in_=s1_perm[4 * e : P, :].bitcast(I32))
-        nc.sync.dma_start(out=w2_sb[:].bitcast(I32), in_=w2_words.rearrange("e s p b -> p (e s) b").bitcast(I32))
+            nc.sync.dma_start(out=s1_planes[e][0:112, :].bitcast(I32), in_=s1_perm[4 * e : 4 * e + 112, :].bitcast(I32))
+        s2_planes = keep.tile([P, E, N], U8, name="s2_planes", tag="scale_rows", align_bytes=64)
+        nc.vector.memset(s2_planes[:].rearrange("p e n -> p (e n)").bitcast(I32), 0)
         for q in range(4):
             nc.sync.dma_start(out=s2_planes[32 * q : 32 * q + 4, :, :].bitcast(I32), in_=s2_i32[4 * q : 4 * q + 4, :, :])
         nc.sync.dma_start(pos1_sb[:], pos1)
         nc.sync.dma_start(pos2_sb[:], pos2)
-        nc.sync.dma_start(out=gate_sb[:], in_=gate.rearrange("r p t -> p r t"))
-
-        def reorder_w1(engine, dst, lo, hi):
-            engine.tensor_copy(
-                out=dst.rearrange("p e b -> p (e b)").bitcast(U16).rearrange("p (e t m) -> p e t m", e=hi - lo, t=4),
-                in_=w1_raw[:, lo:hi, :].rearrange("p e b -> p (e b)").bitcast(U16).rearrange("p (e m t) -> p e t m", e=hi - lo, t=4),
-            )
 
         def round_block(block):
-            lo = block * X_BLOCK
+            lo, hi = X_EDGES[block], X_EDGES[block + 1]
             cut = lo + VECTOR_SHARE[block]
-            for copy, a, b in ((nc.vector.tensor_copy, lo, cut), (nc.scalar.copy, cut, lo + X_BLOCK)):
+            for copy, a, b in ((nc.vector.tensor_copy, lo, cut), (nc.scalar.copy, cut, hi)):
                 copy(
                     out=x_bf[:, a:b, :].rearrange("p (c i) j -> p c j i", i=4),
-                    in_=x_raw[:, :, a:b].rearrange("p j (c i) -> p c j i", i=4),
+                    in_=x_raw[block][:, :, a - lo : b - lo].rearrange("p j (c i) -> p c j i", i=4),
                 )
 
         def quantize_block(block):
-            tokens = slice(block * X_BLOCK, (block + 1) * X_BLOCK)
+            tokens = slice(X_EDGES[block], X_EDGES[block + 1])
             nc.vector.quantize_mx(
                 out=x_codes[:, tokens].bitcast(FP8X4),
                 scales=x_scales[:, tokens],
                 in_=x_bf[:, tokens, :].rearrange("p t j -> p (t j)"),
             )
 
-        reorder_w1(nc.vector, w1_early[:], 0, 2)
         round_block(0)
-        round_block(1)
         quantize_block(0)
+        round_block(1)
         round_block(2)
         quantize_block(1)
+        round_block(3)
         quantize_block(2)
-        w1_late = keep.tile([P, 2, 2 * H], U8, name="w1_late", tag="turns", align_bytes=64)
-        reorder_w1(nc.gpsimd, w1_late[:, 0:1, :], 2, 3)
-        reorder_w1(nc.gpsimd, w1_late[:, 1:2, :], 3, 4)
-        w1_perm = [w1_early[:, 0, :], w1_early[:, 1, :], w1_late[:, 0, :], w1_late[:, 1, :]]
+        quantize_block(3)
+        w2_sb = keep.tile([P, E, 2 * N], U8, name="w2_sb", tag="x2", align_bytes=64)
+        nc.sync.dma_start(out=w2_sb[:].bitcast(I32), in_=w2_words.rearrange("e s p b -> p (e s) b").bitcast(I32))
+        gate_sb = keep.tile([P, 2, T], F32, name="gate_sb", tag="x3", align_bytes=64)
+        nc.sync.dma_start(out=gate_sb[:], in_=gate.rearrange("r p t -> p r t"))
+        w1_late = keep.tile([P, E * H], U16, name="w1_late", tag="turns", align_bytes=64)
+        for e, lo, hi in [(0, 0, 2), (0, 2, 4)] + [(e, 0, 4) for e in range(1, E)]:
+            nc.gpsimd.tensor_copy(
+                out=w1_late[:, e * H + lo * P : e * H + hi * P].rearrange("p (t m) -> p t m", m=P),
+                in_=w1_raw[:, e, :].bitcast(U16).rearrange("p (m t) -> p t m", t=4)[:, lo:hi, :],
+            )
 
         g_codes = keep.tile([P, S], U32, name="g_codes", align_bytes=64)
         g_scales = keep.tile([P, S], U8, name="g_scales", align_bytes=64)
@@ -145,7 +147,7 @@ def tile_moe_cap2_mlp_gelu_kernel(tc, xT, w1_words, w1_scales, w2_words, w2_scal
             for t in range(4):
                 nc.tensor.matmul_mx(
                     out=bank[:, t * U : (t + 1) * U],
-                    lhsT=w1_perm[e][:, t * 2 * P : (t + 1) * 2 * P].bitcast(FP4X4),
+                    lhsT=w1_late[:, e * H + t * P : e * H + (t + 1) * P].bitcast(FP4X4),
                     lhsT_scale=s1_planes[e][:, t * P : (t + 1) * P],
                     rhs=g_codes[:, slots].bitcast(FP8X4),
                     rhs_scale=g_scales[:, slots],
@@ -191,14 +193,18 @@ def tile_moe_cap2_mlp_gelu_kernel(tc, xT, w1_words, w1_scales, w2_words, w2_scal
         def pick(dst, pos_sb, choice, lo, hi):
             nc.vector.tensor_tensor(dst[:, lo:hi], y_sb[:].indirect(pos_sb[:, lo // LIST : hi // LIST]), gate_sb[:, choice, lo:hi], ALU.mult)
 
-        def finish(lo, hi):
+        def add(lo, hi):
             nc.vector.tensor_add(out_sb[:, lo:hi], first_sb[:, lo:hi], second_sb[:, lo:hi])
+
+        def store(lo, hi):
             nc.sync.dma_start(out=out[:, lo:hi], in_=out_sb[:, lo:hi])
 
         pick(first_sb, pos1_sb, 0, 0, OUT_FIRST)
         pick(second_sb, pos2_sb, 1, 0, OUT_FIRST)
         pick(first_sb, pos1_sb, 0, OUT_FIRST, T)
-        finish(0, OUT_EARLY)
+        add(0, OUT_EARLY)
+        store(0, OUT_EARLY)
         pick(second_sb, pos2_sb, 1, OUT_FIRST, T)
-        finish(OUT_EARLY, OUT_FIRST)
-        finish(OUT_FIRST, T)
+        add(OUT_EARLY, OUT_FIRST)
+        add(OUT_FIRST, T)
+        store(OUT_EARLY, T)

@@ -70,13 +70,13 @@ def tile_moe_cap2_mlp_gelu_kernel(tc, xT, w1_words, w1_scales, w2_words, w2_scal
             lo, hi = X_EDGES[block], X_EDGES[block + 1]
             nc.sync.dma_start(out=x_raw[block][:], in_=x_view[:, :, lo:hi])
 
+        load_w1(0, 1)
         for q in range(4):
             nc.sync.dma_start(out=s1_rows[32 * q : 32 * q + 4 * E, :], in_=s1_i32[:, 4 * q : 4 * q + 4, :])
         nc.scalar.activation(out=y_sb[:, S : S + PAD], in_=zeros[:], func=ACT.Gelu_apprx_tanh)
 
         for block in range(4):
             load_x(block)
-        load_w1(0, 1)
         nc.sync.dma_start(offs_sb[:], offs)
         load_w1(1, 4)
 
@@ -112,6 +112,14 @@ def tile_moe_cap2_mlp_gelu_kernel(tc, xT, w1_words, w1_scales, w2_words, w2_scal
                 in_=x_bf[:, tokens, :].rearrange("p t j -> p (t j)"),
             )
 
+        def reorder_w1(engine, dst, e):
+            engine.tensor_copy(
+                out=dst.rearrange("p (t m) -> p t m", m=P),
+                in_=w1_raw[:, e, :].bitcast(U16).rearrange("p (m t) -> p t m", t=4),
+            )
+
+        w1_first = keep.tile([P, H], U16, name="w1_first", align_bytes=64)
+        reorder_w1(nc.vector, w1_first[:], 0)
         round_block(0)
         quantize_block(0)
         round_block(1)
@@ -124,12 +132,10 @@ def tile_moe_cap2_mlp_gelu_kernel(tc, xT, w1_words, w1_scales, w2_words, w2_scal
         nc.sync.dma_start(out=w2_sb[:].bitcast(I32), in_=w2_words.rearrange("e s p b -> p (e s) b").bitcast(I32))
         gate_sb = keep.tile([P, 2, T], F32, name="gate_sb", tag="x3", align_bytes=64)
         nc.sync.dma_start(out=gate_sb[:], in_=gate.rearrange("r p t -> p r t"))
-        w1_late = keep.tile([P, E * H], U16, name="w1_late", tag="turns", align_bytes=64)
-        for e, lo, hi in [(0, 0, 2), (0, 2, 4)] + [(e, 0, 4) for e in range(1, E)]:
-            nc.gpsimd.tensor_copy(
-                out=w1_late[:, e * H + lo * P : e * H + hi * P].rearrange("p (t m) -> p t m", m=P),
-                in_=w1_raw[:, e, :].bitcast(U16).rearrange("p (m t) -> p t m", t=4)[:, lo:hi, :],
-            )
+        w1_late = keep.tile([P, (E - 1) * H], U16, name="w1_late", tag="turns", align_bytes=64)
+        w1_perm = [w1_first[:]] + [w1_late[:, (e - 1) * H : e * H] for e in range(1, E)]
+        for e in range(1, E):
+            reorder_w1(nc.gpsimd, w1_perm[e], e)
 
         g_codes = keep.tile([P, S], U32, name="g_codes", align_bytes=64)
         g_scales = keep.tile([P, S], U8, name="g_scales", align_bytes=64)
@@ -147,7 +153,7 @@ def tile_moe_cap2_mlp_gelu_kernel(tc, xT, w1_words, w1_scales, w2_words, w2_scal
             for t in range(4):
                 nc.tensor.matmul_mx(
                     out=bank[:, t * U : (t + 1) * U],
-                    lhsT=w1_late[:, e * H + t * P : e * H + (t + 1) * P].bitcast(FP4X4),
+                    lhsT=w1_perm[e][:, t * P : (t + 1) * P].bitcast(FP4X4),
                     lhsT_scale=s1_planes[e][:, t * P : (t + 1) * P],
                     rhs=g_codes[:, slots].bitcast(FP8X4),
                     rhs_scale=g_scales[:, slots],

@@ -9,12 +9,13 @@ P = 128
 U = 128
 UNITS = S // U
 LIST = 16
+SHIFTED = 112
 
-X_EDGES = (0, 256, 512, 640, 768)
-X_BLOCK = 256
-VECTOR_SHARE = (160, 192, 32, 96)
-OUT_FIRST = 640
-OUT_EARLY = 512
+LOAD_EDGES = (0, 128, 256, 512, 640, 768)
+VECTOR_SHARE = (0, 0, 192, 32, 96)
+QUANT_EDGES = (0, 256, 512, 640, 768)
+OUT_FIRST = 576
+OUT_EARLY = 384
 
 F32 = mybir.dt.float32
 BF16 = mybir.dt.bfloat16
@@ -36,16 +37,17 @@ def tile_moe_cap2_mlp_gelu_kernel(tc, xT, w1_words, w1_scales, w2_words, w2_scal
         keep = ctx.enter_context(tc.tile_pool(name="keep", bufs=1))
         psum = ctx.enter_context(tc.psum_pool(name="psum", bufs=UNITS))
 
+        loads = list(zip(LOAD_EDGES, LOAD_EDGES[1:]))
         offs_sb = keep.tile([P, S // LIST], U16, name="offs_sb")
         pos1_sb = keep.tile([P, T // LIST], U16, name="pos1_sb")
         pos2_sb = keep.tile([P, T // LIST], U16, name="pos2_sb")
-        x_raw = [keep.tile([P, 4, hi - lo], F32, name="x_raw%d" % b, tag="x%d" % b, align_bytes=64) for b, (lo, hi) in enumerate(zip(X_EDGES, X_EDGES[1:]))]
-        x_bf = keep.tile([P, T, 4], BF16, name="x_bf", tag="turns", align_bytes=64)
+        x_raw = [keep.tile([P, 4, hi - lo], F32, name="x_raw%d" % b, tag="x_raw%d" % b, align_bytes=64) for b, (lo, hi) in enumerate(loads)]
+        x_bf = keep.tile([P, T, 4], BF16, name="x_bf", tag="x_bf", align_bytes=64)
         x_codes = keep.tile([P, T], U32, name="x_codes", align_bytes=64)
         x_scales = keep.tile([P, T], U8, name="x_scales", align_bytes=64)
-        w1_raw = keep.tile([P, E, 2 * H], U8, name="w1_raw", align_bytes=64)
+        w1_raw = [keep.tile([P, 2 * H], U8, name="w1_raw%d" % e, tag="w1_raw%d" % e, align_bytes=64) for e in range(E)]
         s1_rows = keep.tile([P, H // 4], I32, name="s1_rows", align_bytes=64)
-        s1_raw = keep.tile([P, H], U8, name="s1_raw", tag="scale_rows", align_bytes=64)
+        s1_raw = keep.tile([P, H], U8, name="s1_raw", align_bytes=64)
         s1_perm = keep.tile([P, H], U8, name="s1_perm", align_bytes=64)
         s1_planes = [s1_perm] + [keep.tile([P, H], U8, name="s1_plane%d" % e, align_bytes=64) for e in range(1, E)]
         y_sb = keep.tile([P, S + PAD], F32, name="y_sb")
@@ -63,22 +65,23 @@ def tile_moe_cap2_mlp_gelu_kernel(tc, xT, w1_words, w1_scales, w2_words, w2_scal
         s1_i32 = w1_scales.rearrange("e s g h -> (e s) g h").bitcast(I32)
         s2_i32 = w2_scales.rearrange("e s g n -> g (e s) n").bitcast(I32)
 
-        def load_w1(lo, hi):
-            nc.sync.dma_start(out=w1_raw[:, lo:hi, :].bitcast(I32), in_=w1_i32[:, lo:hi, :])
+        def load_x(b):
+            lo, hi = loads[b]
+            nc.sync.dma_start(out=x_raw[b][:], in_=x_view[:, :, lo:hi])
 
-        def load_x(block):
-            lo, hi = X_EDGES[block], X_EDGES[block + 1]
-            nc.sync.dma_start(out=x_raw[block][:], in_=x_view[:, :, lo:hi])
+        def load_w1(e):
+            nc.sync.dma_start(out=w1_raw[e][:].bitcast(I32), in_=w1_i32[:, e, :])
 
-        load_w1(0, 1)
+        load_x(0)
         for q in range(4):
             nc.sync.dma_start(out=s1_rows[32 * q : 32 * q + 4 * E, :], in_=s1_i32[:, 4 * q : 4 * q + 4, :])
         nc.scalar.activation(out=y_sb[:, S : S + PAD], in_=zeros[:], func=ACT.Gelu_apprx_tanh)
-
-        for block in range(4):
-            load_x(block)
+        for b in range(1, len(loads)):
+            load_x(b)
+        load_w1(0)
         nc.sync.dma_start(offs_sb[:], offs)
-        load_w1(1, 4)
+        for e in range(1, E):
+            load_w1(e)
 
         for q in range(4):
             nc.vector.tensor_copy(out=s1_raw[32 * q : 32 * q + 4 * E, :].bitcast(I32), in_=s1_rows[32 * q : 32 * q + 4 * E, :])
@@ -87,55 +90,66 @@ def tile_moe_cap2_mlp_gelu_kernel(tc, xT, w1_words, w1_scales, w2_words, w2_scal
             in_=s1_raw[:].rearrange("p (m t) -> p t m", t=4),
         )
         for e in range(1, E):
-            nc.sync.dma_start(out=s1_planes[e][0:112, :].bitcast(I32), in_=s1_perm[4 * e : 4 * e + 112, :].bitcast(I32))
-        s2_planes = keep.tile([P, E, N], U8, name="s2_planes", tag="scale_rows", align_bytes=64)
-        nc.vector.memset(s2_planes[:].rearrange("p e n -> p (e n)").bitcast(I32), 0)
-        for q in range(4):
-            nc.sync.dma_start(out=s2_planes[32 * q : 32 * q + 4, :, :].bitcast(I32), in_=s2_i32[4 * q : 4 * q + 4, :, :])
+            nc.sync.dma_start(out=s1_planes[e][0:SHIFTED, :].bitcast(I32), in_=s1_perm[4 * e : 4 * e + SHIFTED, :].bitcast(I32))
         nc.sync.dma_start(pos1_sb[:], pos1)
         nc.sync.dma_start(pos2_sb[:], pos2)
 
-        def round_block(block):
-            lo, hi = X_EDGES[block], X_EDGES[block + 1]
-            cut = lo + VECTOR_SHARE[block]
-            for copy, a, b in ((nc.vector.tensor_copy, lo, cut), (nc.scalar.copy, cut, hi)):
-                copy(
-                    out=x_bf[:, a:b, :].rearrange("p (c i) j -> p c j i", i=4),
-                    in_=x_raw[block][:, :, a - lo : b - lo].rearrange("p j (c i) -> p c j i", i=4),
-                )
+        def round_load(b):
+            lo, hi = loads[b]
+            cut = VECTOR_SHARE[b]
+            for copy, first, last in ((nc.vector.tensor_copy, 0, cut), (nc.scalar.copy, cut, hi - lo)):
+                if last > first:
+                    copy(
+                        out=x_bf[:, lo + first : lo + last, :].rearrange("p (c i) j -> p c j i", i=4),
+                        in_=x_raw[b][:, :, first:last].rearrange("p j (c i) -> p c j i", i=4),
+                    )
 
-        def quantize_block(block):
-            tokens = slice(X_EDGES[block], X_EDGES[block + 1])
+        def quantize_tokens(block):
+            tokens = slice(QUANT_EDGES[block], QUANT_EDGES[block + 1])
             nc.vector.quantize_mx(
                 out=x_codes[:, tokens].bitcast(FP8X4),
                 scales=x_scales[:, tokens],
                 in_=x_bf[:, tokens, :].rearrange("p t j -> p (t j)"),
             )
 
-        def reorder_w1(engine, dst, e):
+        def reorder_w1(engine, dst, e, t_lo, t_hi):
             engine.tensor_copy(
                 out=dst.rearrange("p (t m) -> p t m", m=P),
-                in_=w1_raw[:, e, :].bitcast(U16).rearrange("p (m t) -> p t m", t=4),
+                in_=w1_raw[e][:].bitcast(U16).rearrange("p (m t) -> p t m", t=4)[:, t_lo:t_hi, :],
             )
 
-        w1_first = keep.tile([P, H], U16, name="w1_first", align_bytes=64)
-        reorder_w1(nc.vector, w1_first[:], 0)
-        round_block(0)
-        quantize_block(0)
-        round_block(1)
-        round_block(2)
-        quantize_block(1)
-        round_block(3)
-        quantize_block(2)
-        quantize_block(3)
-        w2_sb = keep.tile([P, E, 2 * N], U8, name="w2_sb", tag="x2", align_bytes=64)
-        nc.sync.dma_start(out=w2_sb[:].bitcast(I32), in_=w2_words.rearrange("e s p b -> p (e s) b").bitcast(I32))
-        gate_sb = keep.tile([P, 2, T], F32, name="gate_sb", tag="x3", align_bytes=64)
-        nc.sync.dma_start(out=gate_sb[:], in_=gate.rearrange("r p t -> p r t"))
-        w1_late = keep.tile([P, (E - 1) * H], U16, name="w1_late", tag="turns", align_bytes=64)
-        w1_perm = [w1_first[:]] + [w1_late[:, (e - 1) * H : e * H] for e in range(1, E)]
+        w1_first = keep.tile([P, 2 * P], U16, name="w1_first", align_bytes=64)
+        round_load(0)
+        round_load(1)
+        quantize_tokens(0)
+        round_load(2)
+        round_load(3)
+        quantize_tokens(1)
+        round_load(4)
+        quantize_tokens(2)
+        quantize_tokens(3)
+        reorder_w1(nc.vector, w1_first[:], 0, 0, 2)
+
+        w2_sb = keep.tile([P, E, 2 * N], U8, name="w2_sb", tag="x_raw3", align_bytes=64)
+        for e in range(E):
+            nc.sync.dma_start(out=w2_sb[:, e, :].bitcast(I32), in_=w2_words[e, 0].bitcast(I32))
+        gate_sb = keep.tile([P, 2, T], F32, name="gate_sb", tag="x_raw4", align_bytes=64)
+        for choice in range(2):
+            nc.sync.dma_start(out=gate_sb[:, choice, :], in_=gate[choice])
+
+        w1_rest = keep.tile([P, E * H - 2 * P], U16, name="w1_rest", tag="x_bf", align_bytes=64)
+        reorder_w1(nc.gpsimd, w1_rest[:, 0 : 2 * P], 0, 2, 4)
         for e in range(1, E):
-            reorder_w1(nc.gpsimd, w1_perm[e], e)
+            reorder_w1(nc.gpsimd, w1_rest[:, e * H - 2 * P : (e + 1) * H - 2 * P], e, 0, 4)
+
+        s2_planes = keep.tile([P, E, N], U8, name="s2_planes", tag="w1_raw1", align_bytes=64)
+        nc.gpsimd.memset(s2_planes[:].rearrange("p e n -> p (e n)").bitcast(I32), 0)
+        for q in range(4):
+            nc.sync.dma_start(out=s2_planes[32 * q : 32 * q + 4, :, :].bitcast(I32), in_=s2_i32[4 * q : 4 * q + 4, :, :])
+
+        def w1_columns(e, t):
+            at = e * H + t * P
+            return w1_first[:, at : at + P] if at < 2 * P else w1_rest[:, at - 2 * P : at - P]
 
         g_codes = keep.tile([P, S], U32, name="g_codes", align_bytes=64)
         g_scales = keep.tile([P, S], U8, name="g_scales", align_bytes=64)
@@ -153,7 +167,7 @@ def tile_moe_cap2_mlp_gelu_kernel(tc, xT, w1_words, w1_scales, w2_words, w2_scal
             for t in range(4):
                 nc.tensor.matmul_mx(
                     out=bank[:, t * U : (t + 1) * U],
-                    lhsT=w1_perm[e][:, t * P : (t + 1) * P].bitcast(FP4X4),
+                    lhsT=w1_columns(e, t).bitcast(FP4X4),
                     lhsT_scale=s1_planes[e][:, t * P : (t + 1) * P],
                     rhs=g_codes[:, slots].bitcast(FP8X4),
                     rhs_scale=g_scales[:, slots],
@@ -199,18 +213,14 @@ def tile_moe_cap2_mlp_gelu_kernel(tc, xT, w1_words, w1_scales, w2_words, w2_scal
         def pick(dst, pos_sb, choice, lo, hi):
             nc.vector.tensor_tensor(dst[:, lo:hi], y_sb[:].indirect(pos_sb[:, lo // LIST : hi // LIST]), gate_sb[:, choice, lo:hi], ALU.mult)
 
-        def add(lo, hi):
+        def finish(lo, hi):
             nc.vector.tensor_add(out_sb[:, lo:hi], first_sb[:, lo:hi], second_sb[:, lo:hi])
-
-        def store(lo, hi):
             nc.sync.dma_start(out=out[:, lo:hi], in_=out_sb[:, lo:hi])
 
         pick(first_sb, pos1_sb, 0, 0, OUT_FIRST)
         pick(second_sb, pos2_sb, 1, 0, OUT_FIRST)
         pick(first_sb, pos1_sb, 0, OUT_FIRST, T)
-        add(0, OUT_EARLY)
-        store(0, OUT_EARLY)
+        finish(0, OUT_EARLY)
         pick(second_sb, pos2_sb, 1, OUT_FIRST, T)
-        add(OUT_EARLY, OUT_FIRST)
-        add(OUT_FIRST, T)
-        store(OUT_EARLY, T)
+        finish(OUT_EARLY, OUT_FIRST)
+        finish(OUT_FIRST, T)

@@ -9,7 +9,7 @@ P = 128
 U = 128
 UNITS = S // U
 LIST = 16
-SHIFTED = 112
+ROWS = 16
 
 LOAD_EDGES = (0, 128, 256, 512, 640, 768)
 VECTOR_SHARE = (0, 0, 192, 32, 96)
@@ -45,11 +45,10 @@ def tile_moe_cap2_mlp_gelu_kernel(tc, xT, w1_words, w1_scales, w2_words, w2_scal
         x_bf = keep.tile([P, T, 4], BF16, name="x_bf", tag="x_bf", align_bytes=64)
         x_codes = keep.tile([P, T], U32, name="x_codes", align_bytes=64)
         x_scales = keep.tile([P, T], U8, name="x_scales", align_bytes=64)
-        w1_raw = [keep.tile([P, 2 * H], U8, name="w1_raw%d" % e, tag="w1_raw%d" % e, align_bytes=64) for e in range(E)]
-        s1_rows = keep.tile([P, H // 4], I32, name="s1_rows", align_bytes=64)
-        s1_raw = keep.tile([P, H], U8, name="s1_raw", align_bytes=64)
+        w1_raw0 = keep.tile([P, 2 * H], U8, name="w1_raw0", tag="w1_raw0", align_bytes=64)
+        s1_raw = keep.tile([P, H], U8, name="s1_raw", tag="s1_raw", align_bytes=64)
         s1_perm = keep.tile([P, H], U8, name="s1_perm", align_bytes=64)
-        s1_planes = [s1_perm] + [keep.tile([P, H], U8, name="s1_plane%d" % e, align_bytes=64) for e in range(1, E)]
+        s1_planes = keep.tile([P, E * H], U8, name="s1_planes", align_bytes=64)
         y_sb = keep.tile([P, S + PAD], F32, name="y_sb")
         first_sb = keep.tile([P, T], F32, name="first_sb")
         second_sb = keep.tile([P, T], F32, name="second_sb")
@@ -57,12 +56,13 @@ def tile_moe_cap2_mlp_gelu_kernel(tc, xT, w1_words, w1_scales, w2_words, w2_scal
         zeros = keep.tile([P, PAD], F32, name="zeros")
 
         nc.vector.memset(zeros[:], 0.0)
-        nc.vector.memset(s1_raw[:].bitcast(I32), 0)
+        nc.vector.memset(s1_raw[E * ROWS : P, :].bitcast(I32), 0)
+        nc.gpsimd.memset(s1_planes[:].bitcast(I32), 0)
         nc.vector.memset(x_scales[:].bitcast(I32), 0)
 
         x_view = xT.rearrange("(p j) t -> p j t", j=4)
         w1_i32 = w1_words.rearrange("e s p b -> p (e s) b").bitcast(I32)
-        s1_i32 = w1_scales.rearrange("e s g h -> (e s) g h").bitcast(I32)
+        s1_i32 = w1_scales.rearrange("e s g h -> g (e s) h").bitcast(I32)
         s2_i32 = w2_scales.rearrange("e s g n -> g (e s) n").bitcast(I32)
 
         def load_x(b):
@@ -70,29 +70,26 @@ def tile_moe_cap2_mlp_gelu_kernel(tc, xT, w1_words, w1_scales, w2_words, w2_scal
             nc.sync.dma_start(out=x_raw[b][:], in_=x_view[:, :, lo:hi])
 
         def load_w1(e):
-            nc.sync.dma_start(out=w1_raw[e][:].bitcast(I32), in_=w1_i32[:, e, :])
+            nc.sync.dma_start(out=w1_raw[e].bitcast(I32), in_=w1_i32[:, e, :])
 
         load_x(0)
-        for q in range(4):
-            nc.sync.dma_start(out=s1_rows[32 * q : 32 * q + 4 * E, :], in_=s1_i32[:, 4 * q : 4 * q + 4, :])
+        nc.sync.dma_start(out=s1_raw[0 : E * ROWS, :].bitcast(I32), in_=s1_i32)
         nc.scalar.activation(out=y_sb[:, S : S + PAD], in_=zeros[:], func=ACT.Gelu_apprx_tanh)
-        for b in range(1, len(loads)):
+        for b in range(1, len(loads) - 1):
             load_x(b)
+        nc.sync.dma_start(pos1_sb[:], pos1)
+        load_x(len(loads) - 1)
+        w1_raw = [w1_raw0[:]]
         load_w1(0)
         nc.sync.dma_start(offs_sb[:], offs)
-        for e in range(1, E):
-            load_w1(e)
+        nc.sync.dma_start(pos2_sb[:], pos2)
 
-        for q in range(4):
-            nc.vector.tensor_copy(out=s1_raw[32 * q : 32 * q + 4 * E, :].bitcast(I32), in_=s1_rows[32 * q : 32 * q + 4 * E, :])
         nc.vector.tensor_copy(
             out=s1_perm[:].rearrange("p (t m) -> p t m", t=4),
             in_=s1_raw[:].rearrange("p (m t) -> p t m", t=4),
         )
-        for e in range(1, E):
-            nc.sync.dma_start(out=s1_planes[e][0:SHIFTED, :].bitcast(I32), in_=s1_perm[4 * e : 4 * e + SHIFTED, :].bitcast(I32))
-        nc.sync.dma_start(pos1_sb[:], pos1)
-        nc.sync.dma_start(pos2_sb[:], pos2)
+        for q in range(4):
+            nc.sync.dma_start(out=s1_planes[32 * q : 32 * q + 4, :].bitcast(I32), in_=s1_perm[ROWS * q : ROWS * (q + 1), :].bitcast(I32))
 
         def round_load(b):
             lo, hi = loads[b]
@@ -115,12 +112,16 @@ def tile_moe_cap2_mlp_gelu_kernel(tc, xT, w1_words, w1_scales, w2_words, w2_scal
         def reorder_w1(engine, dst, e, t_lo, t_hi):
             engine.tensor_copy(
                 out=dst.rearrange("p (t m) -> p t m", m=P),
-                in_=w1_raw[e][:].bitcast(U16).rearrange("p (m t) -> p t m", t=4)[:, t_lo:t_hi, :],
+                in_=w1_raw[e].bitcast(U16).rearrange("p (m t) -> p t m", t=4)[:, t_lo:t_hi, :],
             )
 
         w1_first = keep.tile([P, 2 * P], U16, name="w1_first", align_bytes=64)
         round_load(0)
         round_load(1)
+        w1_late = keep.tile([P, (E - 1) * 2 * H], U8, name="w1_late", tag="x_raw1", align_bytes=64)
+        for e in range(1, E):
+            w1_raw.append(w1_late[:, (e - 1) * 2 * H : e * 2 * H])
+        nc.sync.dma_start(out=w1_late[:].bitcast(I32).rearrange("p (e b) -> p e b", e=E - 1), in_=w1_i32[:, 1:E, :])
         quantize_tokens(0)
         round_load(2)
         round_load(3)
@@ -131,18 +132,16 @@ def tile_moe_cap2_mlp_gelu_kernel(tc, xT, w1_words, w1_scales, w2_words, w2_scal
         reorder_w1(nc.vector, w1_first[:], 0, 0, 2)
 
         w2_sb = keep.tile([P, E, 2 * N], U8, name="w2_sb", tag="x_raw3", align_bytes=64)
-        for e in range(E):
-            nc.sync.dma_start(out=w2_sb[:, e, :].bitcast(I32), in_=w2_words[e, 0].bitcast(I32))
+        nc.sync.dma_start(out=w2_sb[:].bitcast(I32), in_=w2_words.rearrange("e s p b -> p (e s) b").bitcast(I32))
         gate_sb = keep.tile([P, 2, T], F32, name="gate_sb", tag="x_raw4", align_bytes=64)
-        for choice in range(2):
-            nc.sync.dma_start(out=gate_sb[:, choice, :], in_=gate[choice])
+        nc.sync.dma_start(out=gate_sb[:], in_=gate.rearrange("c p t -> p c t"))
 
         w1_rest = keep.tile([P, E * H - 2 * P], U16, name="w1_rest", tag="x_bf", align_bytes=64)
         reorder_w1(nc.gpsimd, w1_rest[:, 0 : 2 * P], 0, 2, 4)
         for e in range(1, E):
             reorder_w1(nc.gpsimd, w1_rest[:, e * H - 2 * P : (e + 1) * H - 2 * P], e, 0, 4)
 
-        s2_planes = keep.tile([P, E, N], U8, name="s2_planes", tag="w1_raw1", align_bytes=64)
+        s2_planes = keep.tile([P, E, N], U8, name="s2_planes", tag="w1_raw0", align_bytes=64)
         nc.gpsimd.memset(s2_planes[:].rearrange("p e n -> p (e n)").bitcast(I32), 0)
         for q in range(4):
             nc.sync.dma_start(out=s2_planes[32 * q : 32 * q + 4, :, :].bitcast(I32), in_=s2_i32[4 * q : 4 * q + 4, :, :])
@@ -153,6 +152,11 @@ def tile_moe_cap2_mlp_gelu_kernel(tc, xT, w1_words, w1_scales, w2_words, w2_scal
 
         g_codes = keep.tile([P, S], U32, name="g_codes", align_bytes=64)
         g_scales = keep.tile([P, S], U8, name="g_scales", align_bytes=64)
+        nc.vector.memset(g_codes[:, S - U : S].bitcast(I32), 0)
+        nc.vector.memset(g_scales[:, S - U : S].bitcast(I32), 0)
+        idle = psum.tile([P, 4 * U], F32, name="bank")
+        nc.tensor.matmul_mx(out=idle[:, 0:U], lhsT=w1_raw0[:, 0 : 2 * P].bitcast(FP4X4), lhsT_scale=s1_planes[:, 0:P],
+                            rhs=g_codes[:, S - U : S].bitcast(FP8X4), rhs_scale=g_scales[:, S - U : S], start=True, stop=True)
         h = [keep.tile([P, C, 4], BF16, name="h%d" % e, align_bytes=64) for e in range(E)]
         h_codes = [keep.tile([P, C], U32, name="h_codes%d" % e, align_bytes=64) for e in range(E)]
         h_scales = [keep.tile([P, C], U8, name="h_scales%d" % e, align_bytes=64) for e in range(E)]
@@ -168,7 +172,7 @@ def tile_moe_cap2_mlp_gelu_kernel(tc, xT, w1_words, w1_scales, w2_words, w2_scal
                 nc.tensor.matmul_mx(
                     out=bank[:, t * U : (t + 1) * U],
                     lhsT=w1_columns(e, t).bitcast(FP4X4),
-                    lhsT_scale=s1_planes[e][:, t * P : (t + 1) * P],
+                    lhsT_scale=s1_planes[:, e * H + t * P : e * H + (t + 1) * P],
                     rhs=g_codes[:, slots].bitcast(FP8X4),
                     rhs_scale=g_scales[:, slots],
                     start=True,

@@ -11,9 +11,9 @@ UNITS = S // U
 LIST = 16
 ROWS = 16
 
-LOAD_EDGES = (0, 128, 256, 512, 640, 768)
-VECTOR_SHARE = (0, 0, 192, 32, 96)
-QUANT_EDGES = (0, 256, 512, 640, 768)
+LOAD_EDGES = (0, 384, 640, 768)
+VECTOR_SHARE = (256, 144, 96)
+QUANT_EDGES = (0, 256, 384, 640, 768)
 OUT_FIRST = 576
 OUT_EARLY = 384
 
@@ -72,13 +72,12 @@ def tile_moe_cap2_mlp_gelu_kernel(tc, xT, w1_words, w1_scales, w2_words, w2_scal
         def load_w1(e):
             nc.sync.dma_start(out=w1_raw[e].bitcast(I32), in_=w1_i32[:, e, :])
 
-        load_x(0)
         nc.sync.dma_start(out=s1_raw[0 : E * ROWS, :].bitcast(I32), in_=s1_i32)
+        load_x(0)
         nc.scalar.activation(out=y_sb[:, S : S + PAD], in_=zeros[:], func=ACT.Gelu_apprx_tanh)
-        for b in range(1, len(loads) - 1):
-            load_x(b)
         nc.sync.dma_start(pos1_sb[:], pos1)
-        load_x(len(loads) - 1)
+        for b in range(1, len(loads)):
+            load_x(b)
         w1_raw = [w1_raw0[:]]
         load_w1(0)
         nc.sync.dma_start(offs_sb[:], offs)
@@ -117,23 +116,21 @@ def tile_moe_cap2_mlp_gelu_kernel(tc, xT, w1_words, w1_scales, w2_words, w2_scal
 
         w1_first = keep.tile([P, 2 * P], U16, name="w1_first", align_bytes=64)
         round_load(0)
-        round_load(1)
-        w1_late = keep.tile([P, (E - 1) * 2 * H], U8, name="w1_late", tag="x_raw1", align_bytes=64)
+        w1_late = keep.tile([P, (E - 1) * 2 * H], U8, name="w1_late", tag="x_raw0", align_bytes=64)
         for e in range(1, E):
             w1_raw.append(w1_late[:, (e - 1) * 2 * H : e * 2 * H])
-        nc.sync.dma_start(out=w1_late[:].bitcast(I32).rearrange("p (e b) -> p e b", e=E - 1), in_=w1_i32[:, 1:E, :])
-        quantize_tokens(0)
-        round_load(2)
-        round_load(3)
+            load_w1(e)
         quantize_tokens(1)
-        round_load(4)
+        quantize_tokens(0)
+        round_load(1)
+        round_load(2)
         quantize_tokens(2)
         quantize_tokens(3)
         reorder_w1(nc.vector, w1_first[:], 0, 0, 2)
 
-        w2_sb = keep.tile([P, E, 2 * N], U8, name="w2_sb", tag="x_raw3", align_bytes=64)
+        w2_sb = keep.tile([P, E, 2 * N], U8, name="w2_sb", tag="x_raw1", align_bytes=64)
         nc.sync.dma_start(out=w2_sb[:].bitcast(I32), in_=w2_words.rearrange("e s p b -> p (e s) b").bitcast(I32))
-        gate_sb = keep.tile([P, 2, T], F32, name="gate_sb", tag="x_raw4", align_bytes=64)
+        gate_sb = keep.tile([P, 2, T], F32, name="gate_sb", tag="x_raw2", align_bytes=64)
         nc.sync.dma_start(out=gate_sb[:], in_=gate.rearrange("c p t -> p c t"))
 
         w1_rest = keep.tile([P, E * H - 2 * P], U16, name="w1_rest", tag="x_bf", align_bytes=64)

@@ -12,7 +12,7 @@ LIST = 16
 ROWS = 16
 
 LOAD_EDGES = (0, 384, 640, 768)
-VECTOR_SHARE = (256, 144, 96)
+VECTOR_SHARE = (256, 160, 64)
 QUANT_EDGES = (0, 256, 384, 640, 768)
 OUT_FIRST = 576
 OUT_EARLY = 384
@@ -76,18 +76,18 @@ def tile_moe_cap2_mlp_gelu_kernel(tc, xT, w1_words, w1_scales, w2_words, w2_scal
         load_x(0)
         nc.scalar.activation(out=y_sb[:, S : S + PAD], in_=zeros[:], func=ACT.Gelu_apprx_tanh)
         nc.sync.dma_start(pos1_sb[:], pos1)
+        nc.sync.dma_start(pos2_sb[:], pos2)
         for b in range(1, len(loads)):
             load_x(b)
         w1_raw = [w1_raw0[:]]
         load_w1(0)
         nc.sync.dma_start(offs_sb[:], offs)
-        nc.sync.dma_start(pos2_sb[:], pos2)
 
         nc.vector.tensor_copy(
             out=s1_perm[:].rearrange("p (t m) -> p t m", t=4),
             in_=s1_raw[:].rearrange("p (m t) -> p t m", t=4),
         )
-        for q in range(4):
+        for q in (0, 2, 1, 3):
             nc.sync.dma_start(out=s1_planes[32 * q : 32 * q + 4, :].bitcast(I32), in_=s1_perm[ROWS * q : ROWS * (q + 1), :].bitcast(I32))
 
         def round_load(b):
@@ -194,8 +194,8 @@ def tile_moe_cap2_mlp_gelu_kernel(tc, xT, w1_words, w1_scales, w2_words, w2_scal
             )
 
         for unit in range(UNITS):
-            if unit == 0 or unit % 2 == 1:
-                served = 1 if unit in (0, UNITS - 1) else 2
+            if unit % 2 == 0 or unit == UNITS - 1:
+                served = 1 if unit >= UNITS - 2 else 2
                 gather(g_scales, x_scales, unit * U, (unit + served) * U)
             gather(g_codes, x_codes, unit * U, (unit + 1) * U)
             first_layer(unit)

@@ -10,12 +10,12 @@ U = 128
 UNITS = S // U
 LIST = 16
 ROWS = 16
+HALF = U // 2
 
-LOAD_EDGES = (0, 384, 640, 768)
-VECTOR_SHARE = (256, 160, 64)
-QUANT_EDGES = (0, 256, 384, 640, 768)
+LOAD_EDGES = (0, 256, 512, 640, 768)
+VECTOR_SHARE = (96, 192, 32, 96)
 OUT_FIRST = 576
-OUT_EARLY = 384
+OUT_EARLY = 320
 
 F32 = mybir.dt.float32
 BF16 = mybir.dt.bfloat16
@@ -46,7 +46,7 @@ def tile_moe_cap2_mlp_gelu_kernel(tc, xT, w1_words, w1_scales, w2_words, w2_scal
         x_codes = keep.tile([P, T], U32, name="x_codes", align_bytes=64)
         x_scales = keep.tile([P, T], U8, name="x_scales", align_bytes=64)
         w1_raw0 = keep.tile([P, 2 * H], U8, name="w1_raw0", tag="w1_raw0", align_bytes=64)
-        s1_raw = keep.tile([P, H], U8, name="s1_raw", tag="s1_raw", align_bytes=64)
+        s1_raw = keep.tile([P, H], U8, name="s1_raw", align_bytes=64)
         s1_perm = keep.tile([P, H], U8, name="s1_perm", align_bytes=64)
         s1_planes = keep.tile([P, E * H], U8, name="s1_planes", align_bytes=64)
         y_sb = keep.tile([P, S + PAD], F32, name="y_sb")
@@ -69,19 +69,16 @@ def tile_moe_cap2_mlp_gelu_kernel(tc, xT, w1_words, w1_scales, w2_words, w2_scal
             lo, hi = loads[b]
             nc.sync.dma_start(out=x_raw[b][:], in_=x_view[:, :, lo:hi])
 
-        def load_w1(e):
-            nc.sync.dma_start(out=w1_raw[e].bitcast(I32), in_=w1_i32[:, e, :])
-
-        nc.sync.dma_start(out=s1_raw[0 : E * ROWS, :].bitcast(I32), in_=s1_i32)
         load_x(0)
+        nc.sync.dma_start(out=s1_raw[0 : E * ROWS, :].bitcast(I32), in_=s1_i32)
         nc.scalar.activation(out=y_sb[:, S : S + PAD], in_=zeros[:], func=ACT.Gelu_apprx_tanh)
+        load_x(1)
         nc.sync.dma_start(pos1_sb[:], pos1)
-        nc.sync.dma_start(pos2_sb[:], pos2)
-        for b in range(1, len(loads)):
-            load_x(b)
-        w1_raw = [w1_raw0[:]]
-        load_w1(0)
+        load_x(2)
+        load_x(3)
+        nc.sync.dma_start(out=w1_raw0[:].bitcast(I32), in_=w1_i32[:, 0, :])
         nc.sync.dma_start(offs_sb[:], offs)
+        nc.sync.dma_start(pos2_sb[:], pos2)
 
         nc.vector.tensor_copy(
             out=s1_perm[:].rearrange("p (t m) -> p t m", t=4),
@@ -100,8 +97,8 @@ def tile_moe_cap2_mlp_gelu_kernel(tc, xT, w1_words, w1_scales, w2_words, w2_scal
                         in_=x_raw[b][:, :, first:last].rearrange("p j (c i) -> p c j i", i=4),
                     )
 
-        def quantize_tokens(block):
-            tokens = slice(QUANT_EDGES[block], QUANT_EDGES[block + 1])
+        def quantize_load(b):
+            tokens = slice(*loads[b])
             nc.vector.quantize_mx(
                 out=x_codes[:, tokens].bitcast(FP8X4),
                 scales=x_scales[:, tokens],
@@ -117,20 +114,21 @@ def tile_moe_cap2_mlp_gelu_kernel(tc, xT, w1_words, w1_scales, w2_words, w2_scal
         w1_first = keep.tile([P, 2 * P], U16, name="w1_first", align_bytes=64)
         round_load(0)
         w1_late = keep.tile([P, (E - 1) * 2 * H], U8, name="w1_late", tag="x_raw0", align_bytes=64)
-        for e in range(1, E):
-            w1_raw.append(w1_late[:, (e - 1) * 2 * H : e * 2 * H])
-            load_w1(e)
-        quantize_tokens(1)
-        quantize_tokens(0)
+        w1_raw = [w1_raw0[:]] + [w1_late[:, (e - 1) * 2 * H : e * 2 * H] for e in range(1, E)]
+        nc.sync.dma_start(out=w1_raw[1].bitcast(I32), in_=w1_i32[:, 1, :])
+        nc.sync.dma_start(out=w1_late[:, 2 * H :].bitcast(I32).rearrange("p (e b) -> p e b", e=E - 2), in_=w1_i32[:, 2:E, :])
+        quantize_load(0)
         round_load(1)
         round_load(2)
-        quantize_tokens(2)
-        quantize_tokens(3)
+        quantize_load(1)
+        round_load(3)
+        quantize_load(2)
+        quantize_load(3)
         reorder_w1(nc.vector, w1_first[:], 0, 0, 2)
 
-        w2_sb = keep.tile([P, E, 2 * N], U8, name="w2_sb", tag="x_raw1", align_bytes=64)
+        w2_sb = keep.tile([P, E, 2 * N], U8, name="w2_sb", tag="x_raw2", align_bytes=64)
         nc.sync.dma_start(out=w2_sb[:].bitcast(I32), in_=w2_words.rearrange("e s p b -> p (e s) b").bitcast(I32))
-        gate_sb = keep.tile([P, 2, T], F32, name="gate_sb", tag="x_raw2", align_bytes=64)
+        gate_sb = keep.tile([P, 2, T], F32, name="gate_sb", tag="x_raw3", align_bytes=64)
         nc.sync.dma_start(out=gate_sb[:], in_=gate.rearrange("c p t -> p c t"))
 
         w1_rest = keep.tile([P, E * H - 2 * P], U16, name="w1_rest", tag="x_bf", align_bytes=64)
@@ -138,10 +136,12 @@ def tile_moe_cap2_mlp_gelu_kernel(tc, xT, w1_words, w1_scales, w2_words, w2_scal
         for e in range(1, E):
             reorder_w1(nc.gpsimd, w1_rest[:, e * H - 2 * P : (e + 1) * H - 2 * P], e, 0, 4)
 
-        s2_planes = keep.tile([P, E, N], U8, name="s2_planes", tag="w1_raw0", align_bytes=64)
-        nc.gpsimd.memset(s2_planes[:].rearrange("p e n -> p (e n)").bitcast(I32), 0)
+        s2_raw = keep.tile([P, E, N], U8, name="s2_raw", tag="w1_raw0", align_bytes=64)
+        nc.gpsimd.memset(s2_raw[:].rearrange("p e n -> p (e n)").bitcast(I32), 0)
         for q in range(4):
-            nc.sync.dma_start(out=s2_planes[32 * q : 32 * q + 4, :, :].bitcast(I32), in_=s2_i32[4 * q : 4 * q + 4, :, :])
+            nc.sync.dma_start(out=s2_raw[32 * q : 32 * q + 4, :, :].bitcast(I32), in_=s2_i32[4 * q : 4 * q + 4, :, :])
+        s2_planes = keep.tile([P, E, N], U8, name="s2_planes", align_bytes=64)
+        nc.gpsimd.tensor_copy(out=s2_planes[:].rearrange("p e n -> p (e n)").bitcast(I32), in_=s2_raw[:].rearrange("p e n -> p (e n)").bitcast(I32))
 
         def w1_columns(e, t):
             at = e * H + t * P
@@ -149,11 +149,6 @@ def tile_moe_cap2_mlp_gelu_kernel(tc, xT, w1_words, w1_scales, w2_words, w2_scal
 
         g_codes = keep.tile([P, S], U32, name="g_codes", align_bytes=64)
         g_scales = keep.tile([P, S], U8, name="g_scales", align_bytes=64)
-        nc.vector.memset(g_codes[:, S - U : S].bitcast(I32), 0)
-        nc.vector.memset(g_scales[:, S - U : S].bitcast(I32), 0)
-        idle = psum.tile([P, 4 * U], F32, name="bank")
-        nc.tensor.matmul_mx(out=idle[:, 0:U], lhsT=w1_raw0[:, 0 : 2 * P].bitcast(FP4X4), lhsT_scale=s1_planes[:, 0:P],
-                            rhs=g_codes[:, S - U : S].bitcast(FP8X4), rhs_scale=g_scales[:, S - U : S], start=True, stop=True)
         h = [keep.tile([P, C, 4], BF16, name="h%d" % e, align_bytes=64) for e in range(E)]
         h_codes = [keep.tile([P, C], U32, name="h_codes%d" % e, align_bytes=64) for e in range(E)]
         h_scales = [keep.tile([P, C], U8, name="h_scales%d" % e, align_bytes=64) for e in range(E)]
@@ -175,9 +170,16 @@ def tile_moe_cap2_mlp_gelu_kernel(tc, xT, w1_words, w1_scales, w2_words, w2_scal
                     start=True,
                     stop=True,
                 )
-            nc.scalar.activation(out=h[e][:, half * U : (half + 1) * U, :], in_=bank[:].rearrange("p (t c) -> p c t", t=4), func=ACT.Gelu_apprx_tanh)
+            width = HALF if unit == UNITS - 1 else U
+            for lo in range(0, U, width):
+                nc.scalar.activation(
+                    out=h[e][:, half * U + lo : half * U + lo + width, :],
+                    in_=bank[:].rearrange("p (t c) -> p c t", t=4)[:, lo : lo + width, :],
+                    func=ACT.Gelu_apprx_tanh,
+                )
 
         def second_layer(e, lo, hi, y_psum):
+            start = min(lo, hi - U)
             nc.vector.quantize_mx(
                 out=h_codes[e][:, lo:hi].bitcast(FP8X4),
                 scales=h_scales[e][:, lo:hi],
@@ -187,29 +189,32 @@ def tile_moe_cap2_mlp_gelu_kernel(tc, xT, w1_words, w1_scales, w2_words, w2_scal
                 out=y_psum,
                 lhsT=w2_sb[:, e, :].bitcast(FP4X4),
                 lhsT_scale=s2_planes[:, e, :],
-                rhs=h_codes[e][:, lo:hi].bitcast(FP8X4),
-                rhs_scale=h_scales[e][:, lo:hi],
+                rhs=h_codes[e][:, start:hi].bitcast(FP8X4),
+                rhs_scale=h_scales[e][:, start:hi],
                 start=True,
                 stop=True,
             )
 
         for unit in range(UNITS):
-            if unit % 2 == 0 or unit == UNITS - 1:
-                served = 1 if unit >= UNITS - 2 else 2
+            if unit == 0 or unit % 2 == 1:
+                served = 1 if unit in (0, UNITS - 1) else 2
                 gather(g_scales, x_scales, unit * U, (unit + served) * U)
             gather(g_codes, x_codes, unit * U, (unit + 1) * U)
             first_layer(unit)
 
-        y_banks = [psum.tile([P, 4 * U], F32, name="bank") for b in range(4)]
+        y_banks = [psum.tile([P, 4 * U], F32, name="bank") for b in range(5)]
         second_layer(0, 0, C, y_banks[0][:, 0:C])
-        second_layer(1, 0, C, y_banks[0][:, C : 2 * C])
-        second_layer(2, 0, C, y_banks[1][:, 0:C])
+        second_layer(1, 0, U, y_banks[0][:, C : C + U])
+        second_layer(1, U, C, y_banks[1][:, 0:U])
+        second_layer(2, 0, C, y_banks[1][:, U : U + C])
         second_layer(3, 0, U, y_banks[2][:, 0:U])
-        second_layer(3, U, C, y_banks[3][:, 0:U])
-        nc.scalar.copy(out=y_sb[:, 0 : 2 * C], in_=y_banks[0][:])
-        nc.vector.tensor_copy(out=y_sb[:, 2 * C : 3 * C], in_=y_banks[1][:, 0:C])
+        second_layer(3, U, U + HALF, y_banks[3][:, 0:U])
+        second_layer(3, U + HALF, C, y_banks[4][:, 0:U])
+        nc.scalar.copy(out=y_sb[:, 0 : C + U], in_=y_banks[0][:, 0 : C + U])
+        nc.vector.tensor_copy(out=y_sb[:, C + U : 3 * C], in_=y_banks[1][:, 0 : C + U])
         nc.scalar.copy(out=y_sb[:, 3 * C : S - U], in_=y_banks[2][:, 0:U])
-        nc.scalar.copy(out=y_sb[:, S - U : S], in_=y_banks[3][:, 0:U])
+        nc.scalar.copy(out=y_sb[:, S - U : S - HALF], in_=y_banks[3][:, HALF:U])
+        nc.scalar.copy(out=y_sb[:, S - HALF : S], in_=y_banks[4][:, HALF:U])
 
         def pick(dst, pos_sb, choice, lo, hi):
             nc.vector.tensor_tensor(dst[:, lo:hi], y_sb[:].indirect(pos_sb[:, lo // LIST : hi // LIST]), gate_sb[:, choice, lo:hi], ALU.mult)

@@ -47,8 +47,8 @@ def tile_moe_cap2_mlp_gelu_kernel(tc, xT, w1_words, w1_scales, w2_words, w2_scal
         x_scales = keep.tile([P, T], U8, name="x_scales", align_bytes=64)
         w1_raw0 = keep.tile([P, 2 * H], U8, name="w1_raw0", tag="w1_raw0", align_bytes=64)
         s1_raw = keep.tile([P, H], U8, name="s1_raw", align_bytes=64)
-        s1_perm = keep.tile([P, H], U8, name="s1_perm", align_bytes=64)
-        s1_planes = keep.tile([P, E * H], U8, name="s1_planes", align_bytes=64)
+        rows = keep.tile([P, H + N], U8, name="rows", align_bytes=64)
+        planes = keep.tile([P, E, H + N], U8, name="planes", align_bytes=64)
         y_sb = keep.tile([P, S + PAD], F32, name="y_sb")
         first_sb = keep.tile([P, T], F32, name="first_sb")
         second_sb = keep.tile([P, T], F32, name="second_sb")
@@ -57,7 +57,7 @@ def tile_moe_cap2_mlp_gelu_kernel(tc, xT, w1_words, w1_scales, w2_words, w2_scal
 
         nc.vector.memset(zeros[:], 0.0)
         nc.vector.memset(s1_raw[E * ROWS : P, :].bitcast(I32), 0)
-        nc.gpsimd.memset(s1_planes[:].bitcast(I32), 0)
+        nc.gpsimd.memset(planes[:].rearrange("p e c -> p (e c)").bitcast(I32), 0)
         nc.vector.memset(x_scales[:].bitcast(I32), 0)
 
         x_view = xT.rearrange("(p j) t -> p j t", j=4)
@@ -73,19 +73,23 @@ def tile_moe_cap2_mlp_gelu_kernel(tc, xT, w1_words, w1_scales, w2_words, w2_scal
         nc.sync.dma_start(out=s1_raw[0 : E * ROWS, :].bitcast(I32), in_=s1_i32)
         nc.scalar.activation(out=y_sb[:, S : S + PAD], in_=zeros[:], func=ACT.Gelu_apprx_tanh)
         load_x(1)
-        nc.sync.dma_start(pos1_sb[:], pos1)
+        nc.sync.dma_start(out=rows[0 : E * ROWS, H:].bitcast(I32), in_=s2_i32)
         load_x(2)
         load_x(3)
         nc.sync.dma_start(out=w1_raw0[:].bitcast(I32), in_=w1_i32[:, 0, :])
         nc.sync.dma_start(offs_sb[:], offs)
+        nc.sync.dma_start(pos1_sb[:], pos1)
         nc.sync.dma_start(pos2_sb[:], pos2)
 
         nc.vector.tensor_copy(
-            out=s1_perm[:].rearrange("p (t m) -> p t m", t=4),
+            out=rows[:, 0:H].rearrange("p (t m) -> p t m", t=4),
             in_=s1_raw[:].rearrange("p (m t) -> p t m", t=4),
         )
         for q in (0, 2, 1, 3):
-            nc.sync.dma_start(out=s1_planes[32 * q : 32 * q + 4, :].bitcast(I32), in_=s1_perm[ROWS * q : ROWS * (q + 1), :].bitcast(I32))
+            nc.sync.dma_start(
+                out=planes[32 * q : 32 * q + 4, :, :].rearrange("p e c -> p (e c)").bitcast(I32),
+                in_=rows[ROWS * q : ROWS * (q + 1), :].bitcast(I32),
+            )
 
         def round_load(b):
             lo, hi = loads[b]
@@ -116,7 +120,8 @@ def tile_moe_cap2_mlp_gelu_kernel(tc, xT, w1_words, w1_scales, w2_words, w2_scal
         w1_late = keep.tile([P, (E - 1) * 2 * H], U8, name="w1_late", tag="x_raw0", align_bytes=64)
         w1_raw = [w1_raw0[:]] + [w1_late[:, (e - 1) * 2 * H : e * 2 * H] for e in range(1, E)]
         nc.sync.dma_start(out=w1_raw[1].bitcast(I32), in_=w1_i32[:, 1, :])
-        nc.sync.dma_start(out=w1_late[:, 2 * H :].bitcast(I32).rearrange("p (e b) -> p e b", e=E - 2), in_=w1_i32[:, 2:E, :])
+        nc.sync.dma_start(out=w1_raw[2].bitcast(I32), in_=w1_i32[:, 2, :])
+        nc.sync.dma_start(out=w1_raw[3].bitcast(I32), in_=w1_i32[:, 3, :])
         quantize_load(0)
         round_load(1)
         round_load(2)
@@ -127,21 +132,17 @@ def tile_moe_cap2_mlp_gelu_kernel(tc, xT, w1_words, w1_scales, w2_words, w2_scal
         reorder_w1(nc.vector, w1_first[:], 0, 0, 2)
 
         w2_sb = keep.tile([P, E, 2 * N], U8, name="w2_sb", tag="x_raw2", align_bytes=64)
-        nc.sync.dma_start(out=w2_sb[:].bitcast(I32), in_=w2_words.rearrange("e s p b -> p (e s) b").bitcast(I32))
+        w2_i32 = w2_words.rearrange("e s p b -> p (e s) b").bitcast(I32)
+        for e in (0, 2):
+            nc.sync.dma_start(out=w2_sb[:, e : e + 2, :].bitcast(I32), in_=w2_i32[:, e : e + 2, :])
         gate_sb = keep.tile([P, 2, T], F32, name="gate_sb", tag="x_raw3", align_bytes=64)
-        nc.sync.dma_start(out=gate_sb[:], in_=gate.rearrange("c p t -> p c t"))
+        for choice in range(2):
+            nc.sync.dma_start(out=gate_sb[:, choice, :], in_=gate[choice])
 
         w1_rest = keep.tile([P, E * H - 2 * P], U16, name="w1_rest", tag="x_bf", align_bytes=64)
         reorder_w1(nc.gpsimd, w1_rest[:, 0 : 2 * P], 0, 2, 4)
         for e in range(1, E):
             reorder_w1(nc.gpsimd, w1_rest[:, e * H - 2 * P : (e + 1) * H - 2 * P], e, 0, 4)
-
-        s2_raw = keep.tile([P, E, N], U8, name="s2_raw", tag="w1_raw0", align_bytes=64)
-        nc.gpsimd.memset(s2_raw[:].rearrange("p e n -> p (e n)").bitcast(I32), 0)
-        for q in range(4):
-            nc.sync.dma_start(out=s2_raw[32 * q : 32 * q + 4, :, :].bitcast(I32), in_=s2_i32[4 * q : 4 * q + 4, :, :])
-        s2_planes = keep.tile([P, E, N], U8, name="s2_planes", align_bytes=64)
-        nc.gpsimd.tensor_copy(out=s2_planes[:].rearrange("p e n -> p (e n)").bitcast(I32), in_=s2_raw[:].rearrange("p e n -> p (e n)").bitcast(I32))
 
         def w1_columns(e, t):
             at = e * H + t * P
@@ -164,7 +165,7 @@ def tile_moe_cap2_mlp_gelu_kernel(tc, xT, w1_words, w1_scales, w2_words, w2_scal
                 nc.tensor.matmul_mx(
                     out=bank[:, t * U : (t + 1) * U],
                     lhsT=w1_columns(e, t).bitcast(FP4X4),
-                    lhsT_scale=s1_planes[:, e * H + t * P : e * H + (t + 1) * P],
+                    lhsT_scale=planes[:, e, t * P : (t + 1) * P],
                     rhs=g_codes[:, slots].bitcast(FP8X4),
                     rhs_scale=g_scales[:, slots],
                     start=True,
@@ -188,7 +189,7 @@ def tile_moe_cap2_mlp_gelu_kernel(tc, xT, w1_words, w1_scales, w2_words, w2_scal
             nc.tensor.matmul_mx(
                 out=y_psum,
                 lhsT=w2_sb[:, e, :].bitcast(FP4X4),
-                lhsT_scale=s2_planes[:, e, :],
+                lhsT_scale=planes[:, e, H:],
                 rhs=h_codes[e][:, start:hi].bitcast(FP8X4),
                 rhs_scale=h_scales[e][:, start:hi],
                 start=True,
@@ -202,19 +203,17 @@ def tile_moe_cap2_mlp_gelu_kernel(tc, xT, w1_words, w1_scales, w2_words, w2_scal
             gather(g_codes, x_codes, unit * U, (unit + 1) * U)
             first_layer(unit)
 
-        y_banks = [psum.tile([P, 4 * U], F32, name="bank") for b in range(5)]
+        y_banks = [psum.tile([P, 4 * U], F32, name="bank") for b in range(4)]
         second_layer(0, 0, C, y_banks[0][:, 0:C])
-        second_layer(1, 0, U, y_banks[0][:, C : C + U])
-        second_layer(1, U, C, y_banks[1][:, 0:U])
-        second_layer(2, 0, C, y_banks[1][:, U : U + C])
+        second_layer(1, 0, C, y_banks[0][:, C : 2 * C])
+        second_layer(2, 0, C, y_banks[1][:, 0:C])
         second_layer(3, 0, U, y_banks[2][:, 0:U])
-        second_layer(3, U, U + HALF, y_banks[3][:, 0:U])
-        second_layer(3, U + HALF, C, y_banks[4][:, 0:U])
-        nc.scalar.copy(out=y_sb[:, 0 : C + U], in_=y_banks[0][:, 0 : C + U])
-        nc.vector.tensor_copy(out=y_sb[:, C + U : 3 * C], in_=y_banks[1][:, 0 : C + U])
-        nc.scalar.copy(out=y_sb[:, 3 * C : S - U], in_=y_banks[2][:, 0:U])
-        nc.scalar.copy(out=y_sb[:, S - U : S - HALF], in_=y_banks[3][:, HALF:U])
-        nc.scalar.copy(out=y_sb[:, S - HALF : S], in_=y_banks[4][:, HALF:U])
+        second_layer(3, U, U + HALF, y_banks[2][:, HALF : HALF + U])
+        second_layer(3, U + HALF, C, y_banks[3][:, 0:U])
+        nc.scalar.copy(out=y_sb[:, 0 : 2 * C], in_=y_banks[0][:])
+        nc.scalar.copy(out=y_sb[:, 2 * C : 3 * C], in_=y_banks[1][:, 0:C])
+        nc.vector.tensor_copy(out=y_sb[:, 3 * C : S - HALF], in_=y_banks[2][:, 0 : U + HALF])
+        nc.scalar.copy(out=y_sb[:, S - HALF : S], in_=y_banks[3][:, HALF:U])
 
         def pick(dst, pos_sb, choice, lo, hi):
             nc.vector.tensor_tensor(dst[:, lo:hi], y_sb[:].indirect(pos_sb[:, lo // LIST : hi // LIST]), gate_sb[:, choice, lo:hi], ALU.mult)

@@ -1,6 +1,7 @@
 from contextlib import ExitStack
 
 import concourse.mybir as mybir
+from concourse.masks import make_identity
 
 K, T, E, C, H, N = 512, 768, 4, 256, 512, 128
 PAD = 32
@@ -14,8 +15,8 @@ HALF = U // 2
 
 LOAD_EDGES = (0, 256, 512, 640, 768)
 VECTOR_SHARE = (96, 192, 32, 96)
-OUT_FIRST = 576
-OUT_EARLY = 320
+OUT_TENSOR = 256
+OUT_LAST = 576
 
 F32 = mybir.dt.float32
 BF16 = mybir.dt.bfloat16
@@ -54,11 +55,14 @@ def tile_moe_cap2_mlp_gelu_kernel(tc, xT, w1_words, w1_scales, w2_words, w2_scal
         second_sb = keep.tile([P, T], F32, name="second_sb")
         out_sb = keep.tile([P, T], F32, name="out_sb")
         zeros = keep.tile([P, PAD], F32, name="zeros")
+        identity = keep.tile([P, P], F32, name="identity")
+        turned = keep.tile([P, OUT_TENSOR], F32, name="turned")
 
         nc.vector.memset(zeros[:], 0.0)
         nc.vector.memset(s1_raw[E * ROWS : P, :].bitcast(I32), 0)
         nc.gpsimd.memset(planes[:].rearrange("p e c -> p (e c)").bitcast(I32), 0)
         nc.vector.memset(x_scales[:].bitcast(I32), 0)
+        make_identity(nc, identity[:])
 
         x_view = xT.rearrange("(p j) t -> p j t", j=4)
         w1_i32 = w1_words.rearrange("e s p b -> p (e s) b").bitcast(I32)
@@ -136,8 +140,8 @@ def tile_moe_cap2_mlp_gelu_kernel(tc, xT, w1_words, w1_scales, w2_words, w2_scal
         for e in (0, 2):
             nc.sync.dma_start(out=w2_sb[:, e : e + 2, :].bitcast(I32), in_=w2_i32[:, e : e + 2, :])
         gate_sb = keep.tile([P, 2, T], F32, name="gate_sb", tag="x_raw3", align_bytes=64)
-        for choice in range(2):
-            nc.sync.dma_start(out=gate_sb[:, choice, :], in_=gate[choice])
+        for tokens in (slice(0, OUT_TENSOR), slice(OUT_TENSOR, T)):
+            nc.sync.dma_start(out=gate_sb[:, :, tokens], in_=gate.rearrange("c p t -> p c t")[:, :, tokens])
 
         w1_rest = keep.tile([P, E * H - 2 * P], U16, name="w1_rest", tag="x_bf", align_bytes=64)
         reorder_w1(nc.gpsimd, w1_rest[:, 0 : 2 * P], 0, 2, 4)
@@ -222,10 +226,23 @@ def tile_moe_cap2_mlp_gelu_kernel(tc, xT, w1_words, w1_scales, w2_words, w2_scal
             nc.vector.tensor_add(out_sb[:, lo:hi], first_sb[:, lo:hi], second_sb[:, lo:hi])
             nc.sync.dma_start(out=out[:, lo:hi], in_=out_sb[:, lo:hi])
 
-        pick(first_sb, pos1_sb, 0, 0, OUT_FIRST)
-        pick(second_sb, pos2_sb, 1, 0, OUT_FIRST)
-        pick(first_sb, pos1_sb, 0, OUT_FIRST, T)
-        finish(0, OUT_EARLY)
-        pick(second_sb, pos2_sb, 1, OUT_FIRST, T)
-        finish(OUT_EARLY, OUT_FIRST)
-        finish(OUT_FIRST, T)
+        blocks = [slice(lo, lo + P) for lo in range(0, OUT_TENSOR, P)]
+        summed = [psum.tile([P, 4 * U], F32, name="bank") for tokens in blocks]
+        back = [psum.tile([P, 4 * U], F32, name="bank") for tokens in blocks]
+        pick(first_sb, pos1_sb, 0, 0, OUT_TENSOR)
+        pick(second_sb, pos2_sb, 1, 0, OUT_TENSOR)
+        for products, opens in ((first_sb, True), (second_sb, False)):
+            for bank, tokens in zip(summed, blocks):
+                nc.tensor.matmul(bank[:, 0:P], lhsT=products[:, tokens], rhs=identity[:], is_transpose=True, start=opens, stop=not opens)
+        for bank, tokens in zip(summed, blocks):
+            nc.scalar.copy(out=turned[:, tokens], in_=bank[:, 0:P])
+        for bank, tokens in zip(back, blocks):
+            nc.tensor.transpose(bank[:, 0:P], turned[:, tokens], identity[:])
+        for bank, tokens in zip(back, blocks):
+            nc.scalar.copy(out=out_sb[:, tokens], in_=bank[:, 0:P])
+        nc.scalar.dma_start(out=out[:, 0:OUT_TENSOR], in_=out_sb[:, 0:OUT_TENSOR])
+        pick(first_sb, pos1_sb, 0, OUT_TENSOR, T)
+        pick(second_sb, pos2_sb, 1, OUT_TENSOR, OUT_LAST)
+        pick(second_sb, pos2_sb, 1, OUT_LAST, T)
+        finish(OUT_TENSOR, OUT_LAST)
+        finish(OUT_LAST, T)

@@ -16,7 +16,7 @@ HALF = U // 2
 LOAD_EDGES = (0, 256, 512, 640, 768)
 VECTOR_SHARE = (96, 192, 32, 96)
 OUT_TENSOR = 256
-OUT_LAST = 576
+OUT_LAST = 512
 
 F32 = mybir.dt.float32
 BF16 = mybir.dt.bfloat16
@@ -48,8 +48,8 @@ def tile_moe_cap2_mlp_gelu_kernel(tc, xT, w1_words, w1_scales, w2_words, w2_scal
         x_scales = keep.tile([P, T], U8, name="x_scales", align_bytes=64)
         w1_raw0 = keep.tile([P, 2 * H], U8, name="w1_raw0", tag="w1_raw0", align_bytes=64)
         s1_raw = keep.tile([P, H], U8, name="s1_raw", align_bytes=64)
-        rows = keep.tile([P, H + N], U8, name="rows", align_bytes=64)
-        planes = keep.tile([P, E, H + N], U8, name="planes", align_bytes=64)
+        rows = keep.tile([P, H], U8, name="rows", align_bytes=64)
+        planes = keep.tile([P, E, H], U8, name="planes", align_bytes=64)
         y_sb = keep.tile([P, S + PAD], F32, name="y_sb")
         first_sb = keep.tile([P, T], F32, name="first_sb")
         second_sb = keep.tile([P, T], F32, name="second_sb")
@@ -77,7 +77,6 @@ def tile_moe_cap2_mlp_gelu_kernel(tc, xT, w1_words, w1_scales, w2_words, w2_scal
         nc.sync.dma_start(out=s1_raw[0 : E * ROWS, :].bitcast(I32), in_=s1_i32)
         nc.scalar.activation(out=y_sb[:, S : S + PAD], in_=zeros[:], func=ACT.Gelu_apprx_tanh)
         load_x(1)
-        nc.sync.dma_start(out=rows[0 : E * ROWS, H:].bitcast(I32), in_=s2_i32)
         load_x(2)
         load_x(3)
         nc.sync.dma_start(out=w1_raw0[:].bitcast(I32), in_=w1_i32[:, 0, :])
@@ -124,8 +123,7 @@ def tile_moe_cap2_mlp_gelu_kernel(tc, xT, w1_words, w1_scales, w2_words, w2_scal
         w1_late = keep.tile([P, (E - 1) * 2 * H], U8, name="w1_late", tag="x_raw0", align_bytes=64)
         w1_raw = [w1_raw0[:]] + [w1_late[:, (e - 1) * 2 * H : e * 2 * H] for e in range(1, E)]
         nc.sync.dma_start(out=w1_raw[1].bitcast(I32), in_=w1_i32[:, 1, :])
-        nc.sync.dma_start(out=w1_raw[2].bitcast(I32), in_=w1_i32[:, 2, :])
-        nc.sync.dma_start(out=w1_raw[3].bitcast(I32), in_=w1_i32[:, 3, :])
+        nc.sync.dma_start(out=w1_late[:, 2 * H :].bitcast(I32).rearrange("p (e b) -> p e b", e=E - 2), in_=w1_i32[:, 2:E, :])
         quantize_load(0)
         round_load(1)
         round_load(2)
@@ -137,16 +135,21 @@ def tile_moe_cap2_mlp_gelu_kernel(tc, xT, w1_words, w1_scales, w2_words, w2_scal
 
         w2_sb = keep.tile([P, E, 2 * N], U8, name="w2_sb", tag="x_raw2", align_bytes=64)
         w2_i32 = w2_words.rearrange("e s p b -> p (e s) b").bitcast(I32)
-        for e in (0, 2):
-            nc.sync.dma_start(out=w2_sb[:, e : e + 2, :].bitcast(I32), in_=w2_i32[:, e : e + 2, :])
+        nc.sync.dma_start(out=w2_sb[:].bitcast(I32), in_=w2_i32)
         gate_sb = keep.tile([P, 2, T], F32, name="gate_sb", tag="x_raw3", align_bytes=64)
-        for tokens in (slice(0, OUT_TENSOR), slice(OUT_TENSOR, T)):
-            nc.sync.dma_start(out=gate_sb[:, :, tokens], in_=gate.rearrange("c p t -> p c t")[:, :, tokens])
+        nc.sync.dma_start(out=gate_sb[:], in_=gate.rearrange("c p t -> p c t"))
 
         w1_rest = keep.tile([P, E * H - 2 * P], U16, name="w1_rest", tag="x_bf", align_bytes=64)
         reorder_w1(nc.gpsimd, w1_rest[:, 0 : 2 * P], 0, 2, 4)
         for e in range(1, E):
             reorder_w1(nc.gpsimd, w1_rest[:, e * H - 2 * P : (e + 1) * H - 2 * P], e, 0, 4)
+
+        s2_raw = keep.tile([P, E, N], U8, name="s2_raw", tag="w1_raw0", align_bytes=64)
+        nc.gpsimd.memset(s2_raw[:].rearrange("p e n -> p (e n)").bitcast(I32), 0)
+        for q in range(4):
+            nc.sync.dma_start(out=s2_raw[32 * q : 32 * q + 4, :, :].bitcast(I32), in_=s2_i32[4 * q : 4 * q + 4, :, :])
+        s2_planes = keep.tile([P, E, N], U8, name="s2_planes", align_bytes=64)
+        nc.gpsimd.tensor_copy(out=s2_planes[:].rearrange("p e n -> p (e n)").bitcast(I32), in_=s2_raw[:].rearrange("p e n -> p (e n)").bitcast(I32))
 
         def w1_columns(e, t):
             at = e * H + t * P
@@ -193,7 +196,7 @@ def tile_moe_cap2_mlp_gelu_kernel(tc, xT, w1_words, w1_scales, w2_words, w2_scal
             nc.tensor.matmul_mx(
                 out=y_psum,
                 lhsT=w2_sb[:, e, :].bitcast(FP4X4),
-                lhsT_scale=planes[:, e, H:],
+                lhsT_scale=s2_planes[:, e, :],
                 rhs=h_codes[e][:, start:hi].bitcast(FP8X4),
                 rhs_scale=h_scales[e][:, start:hi],
                 start=True,

@@ -15,8 +15,8 @@ HALF = U // 2
 
 LOAD_EDGES = (0, 256, 512, 640, 768)
 VECTOR_SHARE = (96, 192, 32, 96)
-OUT_TENSOR = 256
-OUT_LAST = 512
+OUT_TENSOR = 384
+OUT_LAST = 640
 
 F32 = mybir.dt.float32
 BF16 = mybir.dt.bfloat16
@@ -204,9 +204,10 @@ def tile_moe_cap2_mlp_gelu_kernel(tc, xT, w1_words, w1_scales, w2_words, w2_scal
             )
 
         for unit in range(UNITS):
-            if unit == 0 or unit % 2 == 1:
-                served = 1 if unit in (0, UNITS - 1) else 2
-                gather(g_scales, x_scales, unit * U, (unit + served) * U)
+            if unit in (1, 3):
+                gather(g_scales, x_scales, unit * U, (unit + 2) * U)
+            elif unit not in (2, 4):
+                gather(g_scales, x_scales, unit * U, (unit + 1) * U)
             gather(g_codes, x_codes, unit * U, (unit + 1) * U)
             first_layer(unit)
 
@@ -233,7 +234,8 @@ def tile_moe_cap2_mlp_gelu_kernel(tc, xT, w1_words, w1_scales, w2_words, w2_scal
         summed = [psum.tile([P, 4 * U], F32, name="bank") for tokens in blocks]
         back = [psum.tile([P, 4 * U], F32, name="bank") for tokens in blocks]
         pick(first_sb, pos1_sb, 0, 0, OUT_TENSOR)
-        pick(second_sb, pos2_sb, 1, 0, OUT_TENSOR)
+        pick(second_sb, pos2_sb, 1, 0, OUT_TENSOR - P)
+        pick(second_sb, pos2_sb, 1, OUT_TENSOR - P, OUT_TENSOR)
         for products, opens in ((first_sb, True), (second_sb, False)):
             for bank, tokens in zip(summed, blocks):
                 nc.tensor.matmul(bank[:, 0:P], lhsT=products[:, tokens], rhs=identity[:], is_transpose=True, start=opens, stop=not opens)
@@ -243,7 +245,8 @@ def tile_moe_cap2_mlp_gelu_kernel(tc, xT, w1_words, w1_scales, w2_words, w2_scal
             nc.tensor.transpose(bank[:, 0:P], turned[:, tokens], identity[:])
         for bank, tokens in zip(back, blocks):
             nc.scalar.copy(out=out_sb[:, tokens], in_=bank[:, 0:P])
-        nc.scalar.dma_start(out=out[:, 0:OUT_TENSOR], in_=out_sb[:, 0:OUT_TENSOR])
+        nc.scalar.dma_start(out=out[:, 0 : OUT_TENSOR - P], in_=out_sb[:, 0 : OUT_TENSOR - P])
+        nc.scalar.dma_start(out=out[:, OUT_TENSOR - P : OUT_TENSOR], in_=out_sb[:, OUT_TENSOR - P : OUT_TENSOR])
         pick(first_sb, pos1_sb, 0, OUT_TENSOR, T)
         pick(second_sb, pos2_sb, 1, OUT_TENSOR, OUT_LAST)
         pick(second_sb, pos2_sb, 1, OUT_LAST, T)

@@ -215,13 +215,13 @@ def tile_moe_cap2_mlp_gelu_kernel(tc, xT, w1_words, w1_scales, w2_words, w2_scal
         second_layer(0, 0, C, y_banks[0][:, 0:C])
         second_layer(1, 0, C, y_banks[0][:, C : 2 * C])
         second_layer(2, 0, C, y_banks[1][:, 0:C])
-        second_layer(3, 0, U, y_banks[2][:, 0:U])
-        second_layer(3, U, U + HALF, y_banks[2][:, HALF : HALF + U])
-        second_layer(3, U + HALF, C, y_banks[3][:, 0:U])
+        second_layer(3, 0, U, y_banks[3][:, 0:U])
+        second_layer(3, U, U + HALF, y_banks[3][:, HALF : HALF + U])
+        second_layer(3, U + HALF, C, y_banks[2][:, 0:U])
         nc.scalar.copy(out=y_sb[:, 0 : 2 * C], in_=y_banks[0][:])
         nc.scalar.copy(out=y_sb[:, 2 * C : 3 * C], in_=y_banks[1][:, 0:C])
-        nc.vector.tensor_copy(out=y_sb[:, 3 * C : S - HALF], in_=y_banks[2][:, 0 : U + HALF])
-        nc.scalar.copy(out=y_sb[:, S - HALF : S], in_=y_banks[3][:, HALF:U])
+        nc.vector.tensor_copy(out=y_sb[:, 3 * C : S - HALF], in_=y_banks[3][:, 0 : U + HALF])
+        nc.scalar.copy(out=y_sb[:, S - HALF : S], in_=y_banks[2][:, HALF:U])
 
         def pick(dst, pos_sb, choice, lo, hi):
             nc.vector.tensor_tensor(dst[:, lo:hi], y_sb[:].indirect(pos_sb[:, lo // LIST : hi // LIST]), gate_sb[:, choice, lo:hi], ALU.mult)
@@ -233,6 +233,16 @@ def tile_moe_cap2_mlp_gelu_kernel(tc, xT, w1_words, w1_scales, w2_words, w2_scal
         blocks = [slice(lo, lo + P) for lo in range(0, OUT_TENSOR, P)]
         summed = [psum.tile([P, 4 * U], F32, name="bank") for tokens in blocks]
         back = [psum.tile([P, 4 * U], F32, name="bank") for tokens in blocks]
+        for t in range(2):
+            nc.tensor.matmul_mx(
+                out=y_banks[2][:],
+                lhsT=w1_columns(0, t).bitcast(FP4X4),
+                lhsT_scale=planes[:, 0, t * P : (t + 1) * P],
+                rhs=g_codes[:, 0 : 4 * U].bitcast(FP8X4),
+                rhs_scale=g_scales[:, 0 : 4 * U],
+                start=True,
+                stop=True,
+            )
         pick(first_sb, pos1_sb, 0, 0, OUT_TENSOR)
         pick(second_sb, pos2_sb, 1, 0, OUT_TENSOR - P)
         pick(second_sb, pos2_sb, 1, OUT_TENSOR - P, OUT_TENSOR)

@@ -1,7 +1,6 @@
 from contextlib import ExitStack
 
 import concourse.mybir as mybir
-from concourse.masks import make_identity
 
 K, T, E, C, H, N = 512, 768, 4, 256, 512, 128
 PAD = 32
@@ -15,8 +14,7 @@ HALF = U // 2
 
 LOAD_EDGES = (0, 256, 512, 640, 768)
 VECTOR_SHARE = (96, 192, 32, 96)
-OUT_TENSOR = 384
-OUT_LAST = 640
+GROUP = 256
 
 F32 = mybir.dt.float32
 BF16 = mybir.dt.bfloat16
@@ -51,18 +49,15 @@ def tile_moe_cap2_mlp_gelu_kernel(tc, xT, w1_words, w1_scales, w2_words, w2_scal
         rows = keep.tile([P, H], U8, name="rows", align_bytes=64)
         planes = keep.tile([P, E, H], U8, name="planes", align_bytes=64)
         y_sb = keep.tile([P, S + PAD], F32, name="y_sb")
-        first_sb = keep.tile([P, T], F32, name="first_sb")
-        second_sb = keep.tile([P, T], F32, name="second_sb")
+        picked = keep.tile([P, 2, T], F32, name="picked")
+        products = keep.tile([P, 2, T], F32, name="products")
         out_sb = keep.tile([P, T], F32, name="out_sb")
         zeros = keep.tile([P, PAD], F32, name="zeros")
-        identity = keep.tile([P, P], F32, name="identity")
-        turned = keep.tile([P, OUT_TENSOR], F32, name="turned")
 
         nc.vector.memset(zeros[:], 0.0)
         nc.vector.memset(s1_raw[E * ROWS : P, :].bitcast(I32), 0)
         nc.gpsimd.memset(planes[:].rearrange("p e c -> p (e c)").bitcast(I32), 0)
         nc.vector.memset(x_scales[:].bitcast(I32), 0)
-        make_identity(nc, identity[:])
 
         x_view = xT.rearrange("(p j) t -> p j t", j=4)
         w1_i32 = w1_words.rearrange("e s p b -> p (e s) b").bitcast(I32)
@@ -223,42 +218,31 @@ def tile_moe_cap2_mlp_gelu_kernel(tc, xT, w1_words, w1_scales, w2_words, w2_scal
         nc.vector.tensor_copy(out=y_sb[:, 3 * C : S - HALF], in_=y_banks[3][:, 0 : U + HALF])
         nc.scalar.copy(out=y_sb[:, S - HALF : S], in_=y_banks[2][:, HALF:U])
 
-        def pick(dst, pos_sb, choice, lo, hi):
-            nc.vector.tensor_tensor(dst[:, lo:hi], y_sb[:].indirect(pos_sb[:, lo // LIST : hi // LIST]), gate_sb[:, choice, lo:hi], ALU.mult)
+        pos_sb = (pos1_sb, pos2_sb)
+        groups = [slice(lo, lo + GROUP) for lo in range(0, T, GROUP)]
 
-        def finish(lo, hi):
-            nc.vector.tensor_add(out_sb[:, lo:hi], first_sb[:, lo:hi], second_sb[:, lo:hi])
-            nc.sync.dma_start(out=out[:, lo:hi], in_=out_sb[:, lo:hi])
+        def results_of(choice, tokens):
+            return y_sb[:].indirect(pos_sb[choice][:, tokens.start // LIST : tokens.stop // LIST])
 
-        blocks = [slice(lo, lo + P) for lo in range(0, OUT_TENSOR, P)]
-        summed = [psum.tile([P, 4 * U], F32, name="bank") for tokens in blocks]
-        back = [psum.tile([P, 4 * U], F32, name="bank") for tokens in blocks]
-        for t in range(2):
-            nc.tensor.matmul_mx(
-                out=y_banks[2][:],
-                lhsT=w1_columns(0, t).bitcast(FP4X4),
-                lhsT_scale=planes[:, 0, t * P : (t + 1) * P],
-                rhs=g_codes[:, 0 : 4 * U].bitcast(FP8X4),
-                rhs_scale=g_scales[:, 0 : 4 * U],
-                start=True,
-                stop=True,
-            )
-        pick(first_sb, pos1_sb, 0, 0, OUT_TENSOR)
-        pick(second_sb, pos2_sb, 1, 0, OUT_TENSOR - P)
-        pick(second_sb, pos2_sb, 1, OUT_TENSOR - P, OUT_TENSOR)
-        for products, opens in ((first_sb, True), (second_sb, False)):
-            for bank, tokens in zip(summed, blocks):
-                nc.tensor.matmul(bank[:, 0:P], lhsT=products[:, tokens], rhs=identity[:], is_transpose=True, start=opens, stop=not opens)
-        for bank, tokens in zip(summed, blocks):
-            nc.scalar.copy(out=turned[:, tokens], in_=bank[:, 0:P])
-        for bank, tokens in zip(back, blocks):
-            nc.tensor.transpose(bank[:, 0:P], turned[:, tokens], identity[:])
-        for bank, tokens in zip(back, blocks):
-            nc.scalar.copy(out=out_sb[:, tokens], in_=bank[:, 0:P])
-        nc.scalar.dma_start(out=out[:, 0 : OUT_TENSOR - P], in_=out_sb[:, 0 : OUT_TENSOR - P])
-        nc.scalar.dma_start(out=out[:, OUT_TENSOR - P : OUT_TENSOR], in_=out_sb[:, OUT_TENSOR - P : OUT_TENSOR])
-        pick(first_sb, pos1_sb, 0, OUT_TENSOR, T)
-        pick(second_sb, pos2_sb, 1, OUT_TENSOR, OUT_LAST)
-        pick(second_sb, pos2_sb, 1, OUT_LAST, T)
-        finish(OUT_TENSOR, OUT_LAST)
-        finish(OUT_LAST, T)
+        def pick_plain(choice, tokens):
+            nc.scalar.activation(picked[:, choice, tokens], results_of(choice, tokens), ACT.Copy)
+
+        def pick_gated(choice, tokens):
+            nc.vector.tensor_tensor(products[:, choice, tokens], results_of(choice, tokens), gate_sb[:, choice, tokens], ALU.mult)
+
+        def apply_gate(choices, tokens):
+            nc.vector.tensor_tensor(products[:, choices, tokens], picked[:, choices, tokens], gate_sb[:, choices, tokens], ALU.mult)
+
+        def finish(tokens):
+            nc.vector.tensor_add(out_sb[:, tokens], products[:, 0, tokens], products[:, 1, tokens])
+            nc.sync.dma_start(out=out[:, tokens], in_=out_sb[:, tokens])
+
+        for tokens in groups:
+            pick_plain(0, tokens)
+        pick_gated(1, slice(0, T))
+        apply_gate(0, groups[0])
+        apply_gate(0, groups[1])
+        finish(groups[0])
+        apply_gate(0, groups[2])
+        finish(groups[1])
+        finish(groups[2])

@@ -107,8 +107,8 @@ def tile_moe_cap2_mlp_gelu_kernel(tc, xT, w1_words, w1_scales, w2_words, w2_scal
                 in_=x_bf[:, tokens, :].rearrange("p t j -> p (t j)"),
             )
 
-        def reorder_w1(engine, dst, e, t_lo, t_hi):
-            engine.tensor_copy(
+        def reorder_w1(copy, dst, e, t_lo, t_hi):
+            copy(
                 out=dst.rearrange("p (t m) -> p t m", m=P),
                 in_=w1_raw[e].bitcast(U16).rearrange("p (m t) -> p t m", t=4)[:, t_lo:t_hi, :],
             )
@@ -126,7 +126,7 @@ def tile_moe_cap2_mlp_gelu_kernel(tc, xT, w1_words, w1_scales, w2_words, w2_scal
         round_load(3)
         quantize_load(2)
         quantize_load(3)
-        reorder_w1(nc.vector, w1_first[:], 0, 0, 2)
+        reorder_w1(nc.scalar.copy, w1_first[:], 0, 0, 2)
 
         w2_sb = keep.tile([P, E, 2 * N], U8, name="w2_sb", tag="x_raw2", align_bytes=64)
         w2_i32 = w2_words.rearrange("e s p b -> p (e s) b").bitcast(I32)
@@ -135,9 +135,9 @@ def tile_moe_cap2_mlp_gelu_kernel(tc, xT, w1_words, w1_scales, w2_words, w2_scal
         nc.sync.dma_start(out=gate_sb[:], in_=gate.rearrange("c p t -> p c t"))
 
         w1_rest = keep.tile([P, E * H - 2 * P], U16, name="w1_rest", tag="x_bf", align_bytes=64)
-        reorder_w1(nc.gpsimd, w1_rest[:, 0 : 2 * P], 0, 2, 4)
+        reorder_w1(nc.gpsimd.tensor_copy, w1_rest[:, 0 : 2 * P], 0, 2, 4)
         for e in range(1, E):
-            reorder_w1(nc.gpsimd, w1_rest[:, e * H - 2 * P : (e + 1) * H - 2 * P], e, 0, 4)
+            reorder_w1(nc.gpsimd.tensor_copy, w1_rest[:, e * H - 2 * P : (e + 1) * H - 2 * P], e, 0, 4)
 
         s2_raw = keep.tile([P, E, N], U8, name="s2_raw", tag="w1_raw0", align_bytes=64)
         nc.gpsimd.memset(s2_raw[:].rearrange("p e n -> p (e n)").bitcast(I32), 0)
@@ -159,10 +159,10 @@ def tile_moe_cap2_mlp_gelu_kernel(tc, xT, w1_words, w1_scales, w2_words, w2_scal
         def gather(dst, src, lo, hi):
             nc.vector.tensor_copy(dst[:, lo:hi], src[:].indirect(offs_sb[:, lo // LIST : hi // LIST]))
 
-        def first_layer(unit):
-            e, half = divmod(unit, 2)
+        def first_layer(lo, hi):
+            e = lo // C
             bank = psum.tile([P, 4 * U], F32, name="bank")
-            slots = slice(unit * U, (unit + 1) * U)
+            slots = slice(hi - U, hi)
             for t in range(4):
                 nc.tensor.matmul_mx(
                     out=bank[:, t * U : (t + 1) * U],
@@ -173,13 +173,11 @@ def tile_moe_cap2_mlp_gelu_kernel(tc, xT, w1_words, w1_scales, w2_words, w2_scal
                     start=True,
                     stop=True,
                 )
-            width = HALF if unit == UNITS - 1 else U
-            for lo in range(0, U, width):
-                nc.scalar.activation(
-                    out=h[e][:, half * U + lo : half * U + lo + width, :],
-                    in_=bank[:].rearrange("p (t c) -> p c t", t=4)[:, lo : lo + width, :],
-                    func=ACT.Gelu_apprx_tanh,
-                )
+            nc.scalar.activation(
+                out=h[e][:, lo - e * C : hi - e * C, :],
+                in_=bank[:].rearrange("p (t c) -> p c t", t=4)[:, U - (hi - lo) : U, :],
+                func=ACT.Gelu_apprx_tanh,
+            )
 
         def second_layer(e, lo, hi, y_psum):
             start = min(lo, hi - U)
@@ -199,12 +197,14 @@ def tile_moe_cap2_mlp_gelu_kernel(tc, xT, w1_words, w1_scales, w2_words, w2_scal
             )
 
         for unit in range(UNITS):
-            if unit in (1, 3):
-                gather(g_scales, x_scales, unit * U, (unit + 2) * U)
-            elif unit not in (2, 4):
+            if unit // 2 == E - 1:
                 gather(g_scales, x_scales, unit * U, (unit + 1) * U)
-            gather(g_codes, x_codes, unit * U, (unit + 1) * U)
-            first_layer(unit)
+            elif unit % 2 == 0:
+                gather(g_scales, x_scales, unit * U, (unit + 2) * U)
+            width = HALF if unit == UNITS - 1 else U
+            for lo in range(unit * U, (unit + 1) * U, width):
+                gather(g_codes, x_codes, lo, lo + width)
+                first_layer(lo, lo + width)
 
         y_banks = [psum.tile([P, 4 * U], F32, name="bank") for b in range(4)]
         second_layer(0, 0, C, y_banks[0][:, 0:C])

@@ -13,7 +13,7 @@ ROWS = 16
 HALF = U // 2
 
 LOAD_EDGES = (0, 256, 512, 640, 768)
-VECTOR_SHARE = (96, 192, 32, 96)
+VECTOR_SHARE = (160, 160, 32, 128)
 GROUP = 256
 
 F32 = mybir.dt.float32

@@ -139,12 +139,9 @@ def tile_moe_cap2_mlp_gelu_kernel(tc, xT, w1_words, w1_scales, w2_words, w2_scal
         for e in range(1, E):
             reorder_w1(nc.gpsimd.tensor_copy, w1_rest[:, e * H - 2 * P : (e + 1) * H - 2 * P], e, 0, 4)
 
-        s2_raw = keep.tile([P, E, N], U8, name="s2_raw", tag="w1_raw0", align_bytes=64)
-        nc.gpsimd.memset(s2_raw[:].rearrange("p e n -> p (e n)").bitcast(I32), 0)
+        s2_planes = rows[:].rearrange("p (e n) -> p e n", e=E)
         for q in range(4):
-            nc.sync.dma_start(out=s2_raw[32 * q : 32 * q + 4, :, :].bitcast(I32), in_=s2_i32[4 * q : 4 * q + 4, :, :])
-        s2_planes = keep.tile([P, E, N], U8, name="s2_planes", align_bytes=64)
-        nc.gpsimd.tensor_copy(out=s2_planes[:].rearrange("p e n -> p (e n)").bitcast(I32), in_=s2_raw[:].rearrange("p e n -> p (e n)").bitcast(I32))
+            nc.sync.dma_start(out=s2_planes[32 * q : 32 * q + 4, :, :].bitcast(I32), in_=s2_i32[4 * q : 4 * q + 4, :, :])
 
         def w1_columns(e, t):
             at = e * H + t * P

@@ -13,7 +13,7 @@ ROWS = 16
 HALF = U // 2
 
 LOAD_EDGES = (0, 256, 512, 640, 768)
-VECTOR_SHARE = (160, 160, 32, 128)
+VECTOR_SHARE = (96, 160, 32, 64)
 GROUP = 256
 
 F32 = mybir.dt.float32

@@ -11,6 +11,7 @@ UNITS = S // U
 LIST = 16
 ROWS = 16
 HALF = U // 2
+ALIGN = 256
 
 LOAD_EDGES = (0, 256, 512, 640, 768)
 VECTOR_SHARE = (96, 160, 32, 64)
@@ -40,19 +41,19 @@ def tile_moe_cap2_mlp_gelu_kernel(tc, xT, w1_words, w1_scales, w2_words, w2_scal
         offs_sb = keep.tile([P, S // LIST], U16, name="offs_sb")
         pos1_sb = keep.tile([P, T // LIST], U16, name="pos1_sb")
         pos2_sb = keep.tile([P, T // LIST], U16, name="pos2_sb")
-        x_raw = [keep.tile([P, 4, hi - lo], F32, name="x_raw%d" % b, tag="x_raw%d" % b, align_bytes=64) for b, (lo, hi) in enumerate(loads)]
-        x_bf = keep.tile([P, T, 4], BF16, name="x_bf", tag="x_bf", align_bytes=64)
-        x_codes = keep.tile([P, T], U32, name="x_codes", align_bytes=64)
-        x_scales = keep.tile([P, T], U8, name="x_scales", align_bytes=64)
-        w1_raw0 = keep.tile([P, 2 * H], U8, name="w1_raw0", tag="w1_raw0", align_bytes=64)
-        s1_raw = keep.tile([P, H], U8, name="s1_raw", align_bytes=64)
-        rows = keep.tile([P, H], U8, name="rows", align_bytes=64)
-        planes = keep.tile([P, E, H], U8, name="planes", align_bytes=64)
-        y_sb = keep.tile([P, S + PAD], F32, name="y_sb")
-        picked = keep.tile([P, 2, T], F32, name="picked")
-        products = keep.tile([P, 2, T], F32, name="products")
-        out_sb = keep.tile([P, T], F32, name="out_sb")
-        zeros = keep.tile([P, PAD], F32, name="zeros")
+        x_raw = [keep.tile([P, 4, hi - lo], F32, name="x_raw%d" % b, tag="x_raw%d" % b, align_bytes=ALIGN) for b, (lo, hi) in enumerate(loads)]
+        x_bf = keep.tile([P, T, 4], BF16, name="x_bf", tag="x_bf", align_bytes=ALIGN)
+        x_codes = keep.tile([P, T], U32, name="x_codes", align_bytes=ALIGN)
+        x_scales = keep.tile([P, T], U8, name="x_scales", align_bytes=ALIGN)
+        w1_raw0 = keep.tile([P, 2 * H], U8, name="w1_raw0", tag="w1_raw0", align_bytes=ALIGN)
+        s1_raw = keep.tile([P, H], U8, name="s1_raw", align_bytes=ALIGN)
+        rows = keep.tile([P, H], U8, name="rows", align_bytes=ALIGN)
+        planes = keep.tile([P, E, H], U8, name="planes", align_bytes=ALIGN)
+        y_sb = keep.tile([P, S + PAD], F32, name="y_sb", align_bytes=ALIGN)
+        picked = keep.tile([P, 2, T], F32, name="picked", align_bytes=ALIGN)
+        products = keep.tile([P, 2, T], F32, name="products", align_bytes=ALIGN)
+        out_sb = keep.tile([P, T], F32, name="out_sb", align_bytes=ALIGN)
+        zeros = keep.tile([P, PAD], F32, name="zeros", align_bytes=ALIGN)
 
         nc.vector.memset(zeros[:], 0.0)
         nc.vector.memset(s1_raw[E * ROWS : P, :].bitcast(I32), 0)
@@ -113,9 +114,9 @@ def tile_moe_cap2_mlp_gelu_kernel(tc, xT, w1_words, w1_scales, w2_words, w2_scal
                 in_=w1_raw[e].bitcast(U16).rearrange("p (m t) -> p t m", t=4)[:, t_lo:t_hi, :],
             )
 
-        w1_first = keep.tile([P, 2 * P], U16, name="w1_first", align_bytes=64)
+        w1_first = keep.tile([P, 2 * P], U16, name="w1_first", align_bytes=ALIGN)
         round_load(0)
-        w1_late = keep.tile([P, (E - 1) * 2 * H], U8, name="w1_late", tag="x_raw0", align_bytes=64)
+        w1_late = keep.tile([P, (E - 1) * 2 * H], U8, name="w1_late", tag="x_raw0", align_bytes=ALIGN)
         w1_raw = [w1_raw0[:]] + [w1_late[:, (e - 1) * 2 * H : e * 2 * H] for e in range(1, E)]
         nc.sync.dma_start(out=w1_raw[1].bitcast(I32), in_=w1_i32[:, 1, :])
         nc.sync.dma_start(out=w1_late[:, 2 * H :].bitcast(I32).rearrange("p (e b) -> p e b", e=E - 2), in_=w1_i32[:, 2:E, :])
@@ -128,13 +129,13 @@ def tile_moe_cap2_mlp_gelu_kernel(tc, xT, w1_words, w1_scales, w2_words, w2_scal
         quantize_load(3)
         reorder_w1(nc.scalar.copy, w1_first[:], 0, 0, 2)
 
-        w2_sb = keep.tile([P, E, 2 * N], U8, name="w2_sb", tag="x_raw2", align_bytes=64)
+        w2_sb = keep.tile([P, E, 2 * N], U8, name="w2_sb", tag="x_raw2", align_bytes=ALIGN)
         w2_i32 = w2_words.rearrange("e s p b -> p (e s) b").bitcast(I32)
         nc.sync.dma_start(out=w2_sb[:].bitcast(I32), in_=w2_i32)
-        gate_sb = keep.tile([P, 2, T], F32, name="gate_sb", tag="x_raw3", align_bytes=64)
+        gate_sb = keep.tile([P, 2, T], F32, name="gate_sb", tag="x_raw3", align_bytes=ALIGN)
         nc.sync.dma_start(out=gate_sb[:], in_=gate.rearrange("c p t -> p c t"))
 
-        w1_rest = keep.tile([P, E * H - 2 * P], U16, name="w1_rest", tag="x_bf", align_bytes=64)
+        w1_rest = keep.tile([P, E * H - 2 * P], U16, name="w1_rest", tag="x_bf", align_bytes=ALIGN)
         reorder_w1(nc.gpsimd.tensor_copy, w1_rest[:, 0 : 2 * P], 0, 2, 4)
         for e in range(1, E):
             reorder_w1(nc.gpsimd.tensor_copy, w1_rest[:, e * H - 2 * P : (e + 1) * H - 2 * P], e, 0, 4)
@@ -147,11 +148,11 @@ def tile_moe_cap2_mlp_gelu_kernel(tc, xT, w1_words, w1_scales, w2_words, w2_scal
             at = e * H + t * P
             return w1_first[:, at : at + P] if at < 2 * P else w1_rest[:, at - 2 * P : at - P]
 
-        g_codes = keep.tile([P, S], U32, name="g_codes", align_bytes=64)
-        g_scales = keep.tile([P, S], U8, name="g_scales", align_bytes=64)
-        h = [keep.tile([P, C, 4], BF16, name="h%d" % e, align_bytes=64) for e in range(E)]
-        h_codes = [keep.tile([P, C], U32, name="h_codes%d" % e, align_bytes=64) for e in range(E)]
-        h_scales = [keep.tile([P, C], U8, name="h_scales%d" % e, align_bytes=64) for e in range(E)]
+        g_codes = keep.tile([P, S], U32, name="g_codes", align_bytes=ALIGN)
+        g_scales = keep.tile([P, S], U8, name="g_scales", align_bytes=ALIGN)
+        h = [keep.tile([P, C, 4], BF16, name="h%d" % e, align_bytes=ALIGN) for e in range(E)]
+        h_codes = [keep.tile([P, C], U32, name="h_codes%d" % e, align_bytes=ALIGN) for e in range(E)]
+        h_scales = [keep.tile([P, C], U8, name="h_scales%d" % e, align_bytes=ALIGN) for e in range(E)]
 
         def gather(dst, src, lo, hi):
             nc.vector.tensor_copy(dst[:, lo:hi], src[:].indirect(offs_sb[:, lo // LIST : hi // LIST]))

from contextlib import ExitStack

import concourse.mybir as mybir

K, T, E, C, H, N = 512, 768, 4, 256, 512, 128
PAD = 32
S = E * C
P = 128
U = 128
UNITS = S // U
LIST = 16
ROWS = 16
HALF = U // 2
ALIGN = 256

LOAD_EDGES = (0, 256, 512, 640, 768)
VECTOR_SHARE = (96, 160, 32, 64)
GROUP = 256

F32 = mybir.dt.float32
BF16 = mybir.dt.bfloat16
I32 = mybir.dt.int32
U32 = mybir.dt.uint32
U16 = mybir.dt.uint16
U8 = mybir.dt.uint8
FP8X4 = mybir.dt.float8_e4m3fn_x4
FP4X4 = mybir.dt.float4_e2m1fn_x4
ACT = mybir.ActivationFunctionType
ALU = mybir.AluOpType

FLOPS = 2 * S * (K * H + H * N)


def tile_moe_cap2_mlp_gelu_kernel(tc, xT, w1_words, w1_scales, w2_words, w2_scales, gate, offs, pos1, pos2, out):
    nc = tc.nc
    with ExitStack() as ctx:
        keep = ctx.enter_context(tc.tile_pool(name="keep", bufs=1))
        psum = ctx.enter_context(tc.psum_pool(name="psum", bufs=UNITS))

        loads = list(zip(LOAD_EDGES, LOAD_EDGES[1:]))
        offs_sb = keep.tile([P, S // LIST], U16, name="offs_sb")
        pos1_sb = keep.tile([P, T // LIST], U16, name="pos1_sb")
        pos2_sb = keep.tile([P, T // LIST], U16, name="pos2_sb")
        x_raw = [keep.tile([P, 4, hi - lo], F32, name="x_raw%d" % b, tag="x_raw%d" % b, align_bytes=ALIGN) for b, (lo, hi) in enumerate(loads)]
        x_bf = keep.tile([P, T, 4], BF16, name="x_bf", tag="x_bf", align_bytes=ALIGN)
        x_codes = keep.tile([P, T], U32, name="x_codes", align_bytes=ALIGN)
        x_scales = keep.tile([P, T], U8, name="x_scales", align_bytes=ALIGN)
        w1_raw0 = keep.tile([P, 2 * H], U8, name="w1_raw0", tag="w1_raw0", align_bytes=ALIGN)
        s1_raw = keep.tile([P, H], U8, name="s1_raw", align_bytes=ALIGN)
        rows = keep.tile([P, H], U8, name="rows", align_bytes=ALIGN)
        planes = keep.tile([P, E, H], U8, name="planes", align_bytes=ALIGN)
        y_sb = keep.tile([P, S + PAD], F32, name="y_sb", align_bytes=ALIGN)
        picked = keep.tile([P, 2, T], F32, name="picked", align_bytes=ALIGN)
        products = keep.tile([P, 2, T], F32, name="products", align_bytes=ALIGN)
        out_sb = keep.tile([P, T], F32, name="out_sb", align_bytes=ALIGN)
        zeros = keep.tile([P, PAD], F32, name="zeros", align_bytes=ALIGN)

        nc.vector.memset(zeros[:], 0.0)
        nc.vector.memset(s1_raw[E * ROWS : P, :].bitcast(I32), 0)
        nc.gpsimd.memset(planes[:].rearrange("p e c -> p (e c)").bitcast(I32), 0)
        nc.vector.memset(x_scales[:].bitcast(I32), 0)

        x_view = xT.rearrange("(p j) t -> p j t", j=4)
        w1_i32 = w1_words.rearrange("e s p b -> p (e s) b").bitcast(I32)
        s1_i32 = w1_scales.rearrange("e s g h -> g (e s) h").bitcast(I32)
        s2_i32 = w2_scales.rearrange("e s g n -> g (e s) n").bitcast(I32)

        def load_x(b):
            lo, hi = loads[b]
            nc.sync.dma_start(out=x_raw[b][:], in_=x_view[:, :, lo:hi])

        load_x(0)
        nc.sync.dma_start(out=s1_raw[0 : E * ROWS, :].bitcast(I32), in_=s1_i32)
        nc.scalar.activation(out=y_sb[:, S : S + PAD], in_=zeros[:], func=ACT.Gelu_apprx_tanh)
        load_x(1)
        load_x(2)
        load_x(3)
        nc.sync.dma_start(out=w1_raw0[:].bitcast(I32), in_=w1_i32[:, 0, :])
        nc.sync.dma_start(offs_sb[:], offs)
        nc.sync.dma_start(pos1_sb[:], pos1)
        nc.sync.dma_start(pos2_sb[:], pos2)

        nc.vector.tensor_copy(
            out=rows[:, 0:H].rearrange("p (t m) -> p t m", t=4),
            in_=s1_raw[:].rearrange("p (m t) -> p t m", t=4),
        )
        for q in (0, 2, 1, 3):
            nc.sync.dma_start(
                out=planes[32 * q : 32 * q + 4, :, :].rearrange("p e c -> p (e c)").bitcast(I32),
                in_=rows[ROWS * q : ROWS * (q + 1), :].bitcast(I32),
            )

        def round_load(b):
            lo, hi = loads[b]
            cut = VECTOR_SHARE[b]
            for copy, first, last in ((nc.vector.tensor_copy, 0, cut), (nc.scalar.copy, cut, hi - lo)):
                if last > first:
                    copy(
                        out=x_bf[:, lo + first : lo + last, :].rearrange("p (c i) j -> p c j i", i=4),
                        in_=x_raw[b][:, :, first:last].rearrange("p j (c i) -> p c j i", i=4),
                    )

        def quantize_load(b):
            tokens = slice(*loads[b])
            nc.vector.quantize_mx(
                out=x_codes[:, tokens].bitcast(FP8X4),
                scales=x_scales[:, tokens],
                in_=x_bf[:, tokens, :].rearrange("p t j -> p (t j)"),
            )

        def reorder_w1(copy, dst, e, t_lo, t_hi):
            copy(
                out=dst.rearrange("p (t m) -> p t m", m=P),
                in_=w1_raw[e].bitcast(U16).rearrange("p (m t) -> p t m", t=4)[:, t_lo:t_hi, :],
            )

        w1_first = keep.tile([P, 2 * P], U16, name="w1_first", align_bytes=ALIGN)
        round_load(0)
        w1_late = keep.tile([P, (E - 1) * 2 * H], U8, name="w1_late", tag="x_raw0", align_bytes=ALIGN)
        w1_raw = [w1_raw0[:]] + [w1_late[:, (e - 1) * 2 * H : e * 2 * H] for e in range(1, E)]
        nc.sync.dma_start(out=w1_raw[1].bitcast(I32), in_=w1_i32[:, 1, :])
        nc.sync.dma_start(out=w1_late[:, 2 * H :].bitcast(I32).rearrange("p (e b) -> p e b", e=E - 2), in_=w1_i32[:, 2:E, :])
        quantize_load(0)
        round_load(1)
        round_load(2)
        quantize_load(1)
        round_load(3)
        quantize_load(2)
        quantize_load(3)
        reorder_w1(nc.scalar.copy, w1_first[:], 0, 0, 2)

        w2_sb = keep.tile([P, E, 2 * N], U8, name="w2_sb", tag="x_raw2", align_bytes=ALIGN)
        w2_i32 = w2_words.rearrange("e s p b -> p (e s) b").bitcast(I32)
        nc.sync.dma_start(out=w2_sb[:].bitcast(I32), in_=w2_i32)
        gate_sb = keep.tile([P, 2, T], F32, name="gate_sb", tag="x_raw3", align_bytes=ALIGN)
        nc.sync.dma_start(out=gate_sb[:], in_=gate.rearrange("c p t -> p c t"))

        w1_rest = keep.tile([P, E * H - 2 * P], U16, name="w1_rest", tag="x_bf", align_bytes=ALIGN)
        reorder_w1(nc.gpsimd.tensor_copy, w1_rest[:, 0 : 2 * P], 0, 2, 4)
        for e in range(1, E):
            reorder_w1(nc.gpsimd.tensor_copy, w1_rest[:, e * H - 2 * P : (e + 1) * H - 2 * P], e, 0, 4)

        s2_planes = rows[:].rearrange("p (e n) -> p e n", e=E)
        for q in range(4):
            nc.sync.dma_start(out=s2_planes[32 * q : 32 * q + 4, :, :].bitcast(I32), in_=s2_i32[4 * q : 4 * q + 4, :, :])

        def w1_columns(e, t):
            at = e * H + t * P
            return w1_first[:, at : at + P] if at < 2 * P else w1_rest[:, at - 2 * P : at - P]

        g_codes = keep.tile([P, S], U32, name="g_codes", align_bytes=ALIGN)
        g_scales = keep.tile([P, S], U8, name="g_scales", align_bytes=ALIGN)
        h = [keep.tile([P, C, 4], BF16, name="h%d" % e, align_bytes=ALIGN) for e in range(E)]
        h_codes = [keep.tile([P, C], U32, name="h_codes%d" % e, align_bytes=ALIGN) for e in range(E)]
        h_scales = [keep.tile([P, C], U8, name="h_scales%d" % e, align_bytes=ALIGN) for e in range(E)]

        def gather(dst, src, lo, hi):
            nc.vector.tensor_copy(dst[:, lo:hi], src[:].indirect(offs_sb[:, lo // LIST : hi // LIST]))

        def first_layer(lo, hi):
            e = lo // C
            bank = psum.tile([P, 4 * U], F32, name="bank")
            slots = slice(hi - U, hi)
            for t in range(4):
                nc.tensor.matmul_mx(
                    out=bank[:, t * U : (t + 1) * U],
                    lhsT=w1_columns(e, t).bitcast(FP4X4),
                    lhsT_scale=planes[:, e, t * P : (t + 1) * P],
                    rhs=g_codes[:, slots].bitcast(FP8X4),
                    rhs_scale=g_scales[:, slots],
                    start=True,
                    stop=True,
                )
            nc.scalar.activation(
                out=h[e][:, lo - e * C : hi - e * C, :],
                in_=bank[:].rearrange("p (t c) -> p c t", t=4)[:, U - (hi - lo) : U, :],
                func=ACT.Gelu_apprx_tanh,
            )

        def second_layer(e, lo, hi, y_psum):
            start = min(lo, hi - U)
            nc.vector.quantize_mx(
                out=h_codes[e][:, lo:hi].bitcast(FP8X4),
                scales=h_scales[e][:, lo:hi],
                in_=h[e][:, lo:hi, :].rearrange("p c t -> p (c t)"),
            )
            nc.tensor.matmul_mx(
                out=y_psum,
                lhsT=w2_sb[:, e, :].bitcast(FP4X4),
                lhsT_scale=s2_planes[:, e, :],
                rhs=h_codes[e][:, start:hi].bitcast(FP8X4),
                rhs_scale=h_scales[e][:, start:hi],
                start=True,
                stop=True,
            )

        for unit in range(UNITS):
            if unit // 2 == E - 1:
                gather(g_scales, x_scales, unit * U, (unit + 1) * U)
            elif unit % 2 == 0:
                gather(g_scales, x_scales, unit * U, (unit + 2) * U)
            width = HALF if unit == UNITS - 1 else U
            for lo in range(unit * U, (unit + 1) * U, width):
                gather(g_codes, x_codes, lo, lo + width)
                first_layer(lo, lo + width)

        y_banks = [psum.tile([P, 4 * U], F32, name="bank") for b in range(4)]
        second_layer(0, 0, C, y_banks[0][:, 0:C])
        second_layer(1, 0, C, y_banks[0][:, C : 2 * C])
        second_layer(2, 0, C, y_banks[1][:, 0:C])
        second_layer(3, 0, U, y_banks[3][:, 0:U])
        second_layer(3, U, U + HALF, y_banks[3][:, HALF : HALF + U])
        second_layer(3, U + HALF, C, y_banks[2][:, 0:U])
        nc.scalar.copy(out=y_sb[:, 0 : 2 * C], in_=y_banks[0][:])
        nc.scalar.copy(out=y_sb[:, 2 * C : 3 * C], in_=y_banks[1][:, 0:C])
        nc.vector.tensor_copy(out=y_sb[:, 3 * C : S - HALF], in_=y_banks[3][:, 0 : U + HALF])
        nc.scalar.copy(out=y_sb[:, S - HALF : S], in_=y_banks[2][:, HALF:U])

        pos_sb = (pos1_sb, pos2_sb)
        groups = [slice(lo, lo + GROUP) for lo in range(0, T, GROUP)]

        def results_of(choice, tokens):
            return y_sb[:].indirect(pos_sb[choice][:, tokens.start // LIST : tokens.stop // LIST])

        def pick_plain(choice, tokens):
            nc.scalar.activation(picked[:, choice, tokens], results_of(choice, tokens), ACT.Copy)

        def pick_gated(choice, tokens):
            nc.vector.tensor_tensor(products[:, choice, tokens], results_of(choice, tokens), gate_sb[:, choice, tokens], ALU.mult)

        def apply_gate(choices, tokens):
            nc.vector.tensor_tensor(products[:, choices, tokens], picked[:, choices, tokens], gate_sb[:, choices, tokens], ALU.mult)

        def finish(tokens):
            nc.vector.tensor_add(out_sb[:, tokens], products[:, 0, tokens], products[:, 1, tokens])
            nc.sync.dma_start(out=out[:, tokens], in_=out_sb[:, tokens])

        for tokens in groups:
            pick_plain(0, tokens)
        pick_gated(1, slice(0, T))
        apply_gate(0, groups[0])
        apply_gate(0, groups[1])
        finish(groups[0])
        apply_gate(0, groups[2])
        finish(groups[1])
        finish(groups[2])
